import numpy as np, ml_dtypes
CORES = [23,119,17,113]
N = 4
BF = ml_dtypes.bfloat16
def gentries(a):
    return np.ascontiguousarray(a.reshape(8, 16, -1).transpose(0, 2, 1)).reshape(8, -1)
def gtable(e):
    e = np.asarray(e); return np.ascontiguousarray(e.reshape(8, -1, 16).transpose(0, 2, 1)).reshape(128, -1).astype(np.int32)
W, L, P, T = 4096, 256, 16, 6
def place(z, e, kap):
    return ((z * (2 * e + 1)[..., None] >> 5) + z + kap) & (W - 1)
def parts(rng):
    low = rng.random((N, 8, 1, W)) < rng.choice(np.array([0.01, 0.03, 0.06, 0.15, 0.5]), (N, 8, 1, 1))
    x = np.where(low, rng.integers(0, 256, (N, 8, 16, W)), rng.integers(64, 256, (N, 8, 16, W)))
    c = rng.integers(0, W, (N, 8, L, 16)); o = rng.integers(0, W, (N, 8, L, P))
    d = np.where(rng.random((N, 8, 1, L)) < 0.5, rng.integers(1, 49, (N, 8, 16, L)), rng.integers(1, 256, (N, 8, 16, L)))
    return x, c, o, d, rng.integers(0, 16, (N, 8, 16, 1))
def pack(x, c, o, d, w):
    return {"xt": np.ascontiguousarray(x.reshape(N, 128, W)).astype(np.float32).astype(BF), "pk": np.stack([gtable(a.reshape(8, -1)) for a in c]), "po": np.stack([gtable(a.reshape(8, -1)) for a in o]),
            "dm": np.ascontiguousarray(d.reshape(N, 128, L)).astype(np.int32), "wt": np.ascontiguousarray(w.reshape(N, 128, 1)).astype(np.int32)}
def setup_inputs(rng):
    return pack(*parts(rng))
def setup_inputs_ties(rng):
    x, c, o, d, w = parts(rng)
    v = rng.integers(8, 200, (N, 8, 16, 1))
    x = v + np.where(rng.random((N, 8, 1, W)) < 0.75, rng.integers(-1, 2, (N, 8, 1, W)), rng.integers(-1, 2, (N, 8, 16, W)))
    d = v + rng.integers(-1, 2, (N, 8, 16, L))
    few = rng.integers(0, W, 8); few[0] = 0; few[7] = W - 1
    c[:, 1::2] = few[rng.integers(0, 8, (N, 4, L, 16))]; o[:, 1::2] = few[rng.integers(0, 8, (N, 4, L, P))]
    return pack(x, c, o, d, w)
def setup_inputs_corners(rng):
    x, c, o, d, w = parts(rng)
    d = rng.choice(np.array([1, 2, 4, 5, 6, 8, 9, 10, 128, 246, 247, 248, 251, 252, 255]), (N, 8, 16, L))
    d[:, :, :, :8] = 1; d[:, :, :, L - 8:] = 255
    x[:, 0] = x[:, 0, :, :1]
    c[:, 1] = c[:, 1, :, :1]; o[:, 1] = o[:, 1, :, :1]
    o[:, 2] = np.concatenate([c[:, 2, :, ::-1]] * (P // 16), axis=2)
    w[:, 3] = 0; w[:, 4] = 15; w[:, 5] = 0; w[:, 5, 15] = rng.integers(1, 16, (N, 1))
    x[:, 6] = 255 * rng.integers(0, 2, (N, 1, W))
    x[:, 7] = rng.integers(0, 256, (N, 16, W)); c[:, 7] = (W - 1) * rng.integers(0, 2, (N, L, 16)); o[:, 7] = (W - 1) * rng.integers(0, 2, (N, L, P))
    q = int(rng.integers(0, N)); x[q] = x[q, :, :, :1]
    return pack(x, c, o, d, w)
def setup_inputs_ends(rng):
    kind = rng.integers(0, 4, (N, 8, 1, W)); hole = rng.integers(0, 16, (N, 8, 1, W))
    x = np.where(kind == 0, 0, np.where(kind == 1, 1, np.where(kind == 2, rng.integers(0, 2, (N, 8, 16, W)), np.arange(16).reshape(16, 1) != hole)))
    w = rng.integers(0, 2, (N, 8, 16, 1)); w[:, 6] = 0; w[:, 7] = 1; w = 15 * w
    kd = rng.integers(0, 4, (N, 8, 1, L)); d = np.where(kd == 0, 0, np.where(kd == 1, 1, rng.integers(0, 2, (N, 8, 16, L))))
    d[:, :, :, L - 1] = 1; d[:, :, :, L - 2] = 0; d = 1 + 254 * d
    c = (W - 1) * rng.integers(0, 2, (N, 8, L, 16)); o = (W - 1) * rng.integers(0, 2, (N, 8, L, P))
    c[:, :, L - 2:] = 0; c[:, :, L - 2:, 15] = W - 1; c[:, :, L - 1, 2] = W - 1
    o[:, :, L - 2:] = W - 1; o[:, :, L - 2:, P - 1] = 0; o[:, :, L - 1, 1] = 0
    c[0, :, :, 7] = W - 1; o[0, :, :, P - 1] = 0; c[0, 3, 5] = 0
    c[N - 1, :, :, 15] = W - 1; o[N - 1, :, :, P - 1] = 0
    m = rng.random((8, L, 1)) < 0.5; c[1] = np.where(m, 0, W - 1); o[1] = np.where(m, o[1], W - 1)
    e = np.add.reduce(w * d, axis=2) & 1023
    p = place(np.full((N, 8, L, 1), W - 1), e, 0)[..., 0]
    tail = int(np.argmax(place(np.arange(W)[None, :], np.zeros(1, np.int64), 0)[0]))
    for q in (0, 1, N - 1):
        for g in range(8): x[q, g][:, p[q, g]] = 1
        x[q, :, :, 0] = 0
    for q in (0, N - 1):
        c[q, 6, L - 2:, 15] = tail; x[q, 6, :, W - 1] = 1
    return pack(255 * x, c, o, d, w)
def setup_inputs_lull(rng):
    x, c, o, d, w = parts(rng)
    q = int(rng.integers(0, N)); p = (q - 1) % N
    x[q] = np.maximum(x[q], 1); x[:, :, :, :32] = 255; x[p, :, :, :32] = 0; x[q, :, :, :32] = 0
    c[p] = 0; o[q, :, :, P - 2:] = 0; o[q] = rng.permuted(o[q], axis=2)
    still = rng.permutation(8 * L)[:int(rng.integers(1, 32))]; c[q, still // L, still % L] = 0
    return pack(x, c, o, d, w)
def setup_inputs_spread(rng):
    x = np.minimum((np.exp2(8 * rng.random((N, 8, 1, W))) * (0.5 + 0.5 * rng.random((N, 8, 16, W)))).astype(np.int64), 255) * (rng.random((N, 8, 1, W)) > 0.0625)
    c = np.minimum((W * rng.random((N, 8, L, 16)) ** 4).astype(np.int64), W - 1); o = np.minimum((W * rng.random((N, 8, L, P)) ** 4).astype(np.int64), W - 1)
    d = np.minimum(np.maximum(np.exp2(8 * rng.random((N, 8, 16, L))).astype(np.int64), 1), 255)
    w = rng.integers(0, 16, (N, 8, 16, 1)) * (rng.random((N, 8, 16, 1)) < 0.4)
    return pack(x, c, o, d, w)
def check_inputs(d):
    bad = []
    for k, lo, hi in (("xt", 0, 255), ("pk", 0, W - 1), ("po", 0, W - 1), ("dm", 1, 255), ("wt", 0, 15)):
        v = np.asarray(d[k]).astype(np.float64)
        if not np.all((v >= lo) & (v <= hi) & (v == np.floor(v))): bad.append("range of " + k)
    return bad
def picks(x, z, e, kap):
    return np.take(x, place(z, e, kap) + (W * np.arange(8 * N)).reshape(N, 8, 1, 1), axis=0)
def reference(xt, pk, po, dm, wt):
    x = np.ascontiguousarray(xt.astype(np.float32).astype(np.int32).reshape(8 * N, 16, W).transpose(0, 2, 1)).reshape(-1, 16)
    c = np.stack([gentries(a) for a in pk]).astype(np.int64).reshape(N, 8, L, 16)
    o = np.stack([gentries(a) for a in po]).astype(np.int64).reshape(N, 8, L, P)
    D = np.ascontiguousarray(dm.astype(np.int32).reshape(N, 8, 16, L).transpose(0, 1, 3, 2))
    w = wt.astype(np.int32).reshape(N, 8, 1, 16)
    kap = np.zeros((N, 1, 1, 1), np.int64); left = []
    for t in range(T):
        if t > 0: c = np.roll(c, 1, axis=0)
        e = (np.add.reduce(w * D, axis=3) & 1023).astype(np.int64)
        a = picks(x, c, e, kap); b = picks(x, o, e, kap)
        if t >= N:
            m = left[t - N]; y = picks(x, m, e, kap); gone = (m != c)[..., None]
            up = np.max(np.where(gone, -1, a), axis=3) >= np.max(np.where(gone, y, -1), axis=3)
            D = np.minimum(np.maximum(np.where(up, D + 8, D - 8), 1), 255)
        sa = np.add.reduce(np.minimum(a, D[:, :, :, None, :]), axis=4); sb = np.add.reduce(np.minimum(b, D[:, :, :, None, :]), axis=4)
        k = np.argmax(sa, axis=3)[..., None]; j = np.argmin(sb, axis=3)[..., None]
        swap = np.take_along_axis(sa, k, 3) > np.take_along_axis(sb, j, 3)
        ck = np.take_along_axis(c, k, 3); oj = np.take_along_axis(o, j, 3)
        np.put_along_axis(c, k, np.where(swap, oj, ck), 3); np.put_along_axis(o, j, np.where(swap, ck, oj), 3)
        xk = np.take_along_axis(a, k[..., None], 3)[:, :, :, 0]
        D = np.where(swap & (xk >= D), np.maximum(D - 4, 1), D)
        kap = np.add.reduce(swap.reshape(N, -1).astype(np.int64), axis=1).reshape(N, 1, 1, 1) & 31
        left.append(c)
    return {"yc": np.stack([gtable(v.reshape(8, -1)) for v in c]).astype(np.float32), "yo": np.stack([gtable(v.reshape(8, -1)) for v in o]).astype(np.float32),
            "yd": np.ascontiguousarray(D.transpose(0, 1, 3, 2)).reshape(N, 128, L).astype(np.float32)}

@@ -1,0 +1,630 @@
+from concourse.mybir import AluOpType as A, ActivationFunctionType as F, AxisListType as AX
+
+W = 4096
+ZC = 4128
+NT = 6
+LEAD = 8
+SCRATCH = {
+    "xt_s": ("sbuf", [128, 4144], "bfloat16"),
+    "wti": ("sbuf", [128, 1], "int32"), "wtf": ("sbuf", [128, 1], "float32"),
+    "dmi": ("sbuf", [128, 8, 32], "int32"),
+    "ci0": ("sbuf", [128, 256], "int32"), "ci1": ("sbuf", [128, 256], "int32"),
+    "cf0": ("sbuf", [128, 256], "float32"), "cf1": ("sbuf", [128, 256], "float32"),
+    "tt0": ("sbuf", [128, 8, 32], "float32"), "tt1": ("sbuf", [128, 8, 32], "float32"),
+    "ywO0": ("sbuf", [128, 128], "float32"), "ywC0": ("sbuf", [128, 128], "float32"),
+    "ywO1": ("sbuf", [128, 128], "float32"), "ywC1": ("sbuf", [128, 128], "float32"),
+    "yO": ("sbuf", [128, 8, 32], "float32"), "yC": ("sbuf", [128, 8, 32], "float32"),
+    "yd_s": ("sbuf", [128, 8, 32], "float32"),
+    "on": ("sbuf", [128, 128], "float32"), "onb": ("sbuf", [128, 128], "bfloat16"),
+    "idf": ("sbuf", [128, 128], "float32"), "idb": ("sbuf", [128, 128], "bfloat16"),
+    "idn": ("sbuf", [128, 128], "bfloat16"), "idm": ("sbuf", [128, 128], "bfloat16"),
+    "shu": ("sbuf", [128, 128], "float32"), "shd": ("sbuf", [128, 128], "float32"),
+    "l00": ("sbuf", [128, 128], "float32"), "l01": ("sbuf", [128, 128], "float32"),
+    "l10": ("sbuf", [128, 128], "float32"), "l11": ("sbuf", [128, 128], "float32"),
+    "blk": ("sbuf", [128, 8], "float32"), "bs": ("sbuf", [128, 8], "float32"), "bw": ("sbuf", [128, 8], "float32"),
+    "pi": ("sbuf", [128, 12], "int32"),
+    "mh": ("sbuf", [128, 4], "float32"), "mh1": ("sbuf", [128, 4], "float32"),
+    "b16i": ("sbuf", [128, 16], "int32"), "b16": ("sbuf", [128, 16], "uint16"), "b8": ("sbuf", [128, 4], "uint16"),
+    "con": ("sbuf", [128, 128], "bfloat16"),
+    "sr": ("sbuf", [128, 2048], "bfloat16"), "wr": ("sbuf", [128, 2048], "bfloat16"),
+    "mkm": ("sbuf", [128, 256], "float32"), "mka": ("sbuf", [128, 128], "float32"),
+    "kc": ("sbuf", [128, 8], "float32"), "kn": ("sbuf", [128, 8], "int32"), "kt": ("sbuf", [128, 8], "float32"),
+}
+for _h in "01":
+    SCRATCH.update({
+        "o" + _h: ("sbuf", [128, 128], "float32"),
+        "d" + _h: ("sbuf", [128, 128], "bfloat16"),
+        "e" + _h: ("sbuf", [128, 8], "float32"), "ei" + _h: ("sbuf", [128, 8], "int32"),
+        "ej" + _h: ("sbuf", [128, 8], "int32"),
+        "drep" + _h: ("psum", [128, 8, 64], "float32"),
+        "bkO" + _h: ("psum", [128, 512], "float32"), "bkC" + _h: ("psum", [128, 512], "float32"),
+        "cps" + _h: ("psum", [128, 512], "float32"),
+        "ks" + _h: ("sbuf", [128, 256], "float32"),
+        "oh" + _h: ("sbuf", [128, 256], "float32"), "sel" + _h: ("sbuf", [128, 256], "float32"),
+        "rs" + _h: ("sbuf", [128, 256], "float32"), "tz" + _h: ("sbuf", [128, 256], "float32"),
+        "sm" + _h: ("sbuf", [128, 80], "float32"),
+        "si" + _h: ("sbuf", [128, 32], "int32"),
+        "sw" + _h: ("sbuf", [128, 8], "bfloat16"),
+        "xo" + _h: ("sbuf", [128, 8], "uint16"),
+        "u" + _h: ("sbuf", [128, 128], "bfloat16"),
+        "aq" + _h: ("sbuf", [128, 48], "int32"),
+        "ai" + _h: ("sbuf", [128, 48], "int32"), "vv" + _h: ("sbuf", [128, 48], "float32"),
+        "gg" + _h: ("sbuf", [128, 48], "float32"), "ne" + _h: ("sbuf", [128, 64], "float32"),
+        "so" + _h: ("sbuf", [128, 48], "uint16"), "sf" + _h: ("sbuf", [128, 48], "float32"),
+        "yg" + _h: ("sbuf", [128, 768], "bfloat16"), "xgi" + _h: ("sbuf", [128, 3, 8, 16], "bfloat16"),
+        "bb" + _h: ("sbuf", [128, 8, 16], "bfloat16"), "up" + _h: ("sbuf", [128, 8, 16], "float32"),
+    })
+    for _l in "OC":
+        SCRATCH.update({
+            "fq" + _l + _h: ("sbuf", [128, 128], "int32"), "f" + _l + _h: ("sbuf", [128, 128], "uint16"),
+            "x" + _l + _h: ("sbuf", [128, 4, 512], "bfloat16"), "mn" + _l + _h: ("sbuf", [128, 8, 256], "bfloat16"),
+            "r" + _l + _h: ("sbuf", [128, 128], "float32"),
+        })
+    SCRATCH["ld" + _h] = ("sbuf", [128, 192 * NT], "float32")
+SEMAPHORES = (["sv", "ss", "sp", "sg", "sent", "lxt", "lwr", "lwt", "ldm", "lpo", "lpk", "oc", "oo", "od"]
+              + ["ar%d%d" % (t, h) for t in range(1, NT) for h in range(2)])
+
+
+def rank_program(g, core, T, topo):
+    rank = T.rank_of(core)
+    if rank is None:
+        return
+    nxt = T.cores[(rank + 1) % len(T.cores)]
+    prv = T.cores[(rank - 1) % len(T.cores)]
+    rid, pid = topo.addr(nxt)[0], topo.addr(nxt)[1]
+    mask = topo.mask(core, nxt)
+    nout, nin = len(topo.engines(core, nxt)), len(topo.engines(prv, core))
+    Q = {"v": g.vector, "s": g.scalar, "p": g.tensor, "g": g, "y": g.sync}
+    S = {"v": T.sem.sv, "s": T.sem.ss, "p": T.sem.sp, "g": T.sem.sg}
+    cnt = {q: 0 for q in Q}
+    known = {q: {} for q in Q}
+    clk, last_w, reads, banks = {}, {}, {}, {}
+
+    def need(q, dep):
+        q2, n = dep
+        if known[q].get(q2, 0) >= n:
+            return
+        Q[q].wait_ge(S[q2], n)
+        known[q][q2] = n
+        for a, m in clk.get(dep, {}).items():
+            if known[q].get(a, 0) < m:
+                known[q][a] = m
+
+    def sync(q, R, Wr, B=()):
+        deps = {}
+        def add(d):
+            if q == "p" and d[0] == "p":
+                return
+            deps[d[0]] = max(deps.get(d[0], 0), d[1])
+        for k in R:
+            if k in last_w:
+                add(last_w[k])
+        for k in Wr:
+            if k in last_w:
+                add(last_w[k])
+            for d in reads.get(k, {}).items():
+                add(d)
+        for b in B:
+            for d in banks.get(b, {}).items():
+                if d[0] != q:
+                    add(d)
+        for d in sorted(deps.items(), key=lambda z: (z[0] == q, z[0])):
+            need(q, d)
+
+    def note(q, n, R, Wr, B=()):
+        for k in R:
+            reads.setdefault(k, {})[q] = n
+        for k in Wr:
+            last_w[k] = (q, n)
+            reads[k] = {}
+        for b in B:
+            banks.setdefault(b, {})[q] = n
+        clk[(q, n)] = dict(known[q])
+
+    buf = [None]
+
+    def later(q, fn):
+        if buf[0] is None:
+            fn()
+        else:
+            buf[0].append((q, fn))
+
+    def seq(*fns):
+        old, buf[0] = buf[0], []
+        for fn in fns:
+            fn[0](*fn[1:])
+        out, buf[0] = buf[0], old
+        return out
+
+    def run(L):
+        for z in L:
+            later(z[0], z[1])
+
+    def split(L, n):
+        k = 0
+        for i, z in enumerate(L):
+            if z[0] == "v":
+                k += 1
+                if k > n:
+                    return L[:i], L[i:]
+        return L, []
+
+    def weave(*Ls):
+        items = []
+        for j, L in enumerate(Ls):
+            nv, k = max(1, sum(1 for z in L if z[0] == "v")), 0
+            for i, z in enumerate(L):
+                if z[0] == "v":
+                    k += 1
+                items.append(((k - 0.5) / nv if k else 0.0, j, i, z))
+        run([z[3] for z in sorted(items, key=lambda z: z[:3])])
+
+    def op(q, name, args, R, Wr, B=(), kw=None):
+        later(q, lambda: op_now(q, name, args, R, Wr, B, kw))
+
+    def op_now(q, name, args, R, Wr, B, kw):
+        sync(q, R, Wr, B)
+        cnt[q] += 1
+        m = {"v": {"tt": g.vector.tensor_tensor, "ts": g.vector.tensor_scalar, "cp": g.vector.tensor_copy,
+                   "ms": g.vector.memset, "red": g.vector.tensor_reduce, "scan": g.vector.tensor_tensor_scan,
+                   "tr": g.vector.transpose},
+             "s": {"act": g.scalar.activation}, "p": {"mm": g.tensor.matmul},
+             "g": {"iota": g.iota, "aff": g.affine_select}}[q][name]
+        m(*args, **(kw or {})).then_inc(S[q], 1)
+        note(q, cnt[q], R, Wr, B)
+
+    def v(name, args, R, Wr, B=(), **kw):
+        op("v", name, args, R, Wr, B, kw)
+
+    def load(q, sem, out, in_, keys):
+        Q[q].dma_start(out, in_).then_inc(T.sem[sem], 16)
+        S[sem] = T.sem[sem]
+        for k in keys:
+            last_w[k] = (sem, 16)
+
+    load("y", "lwt", T.wti[:], T.wt[:], ["wti"])
+    load("y", "ldm", T.dmi[:], T.dm[:], ["dmi"])
+    load("s", "lxt", T.xt_s[:, 0:W], T.xt[:], ["xt.m"])
+    load("y", "lpo", T.ci0[:], T.po[:], ["ci0"])
+    load("y", "lpk", T.ci1[:], T.pk[:], ["ci1"])
+    load("s", "lwr", T.xt_s[:, W:W + 32], T.xt[:, 0:32], ["xt.w"])
+    XTK = ["xt.m", "xt.w", "xt.z"]
+    xtab = T.xt_s[:, 0:4144]
+
+    v("ms", (T.on[:], 1.0), [], ["on"])
+    v("ms", (T.wr[:], 0.0), [], ["wr"])
+    op("g", "aff", (T.blk[:], T.on[:, 0:8], [[-16, 8]], A.is_ge, 0.0, 0, 1), ["on"], ["blk"])
+    op("g", "aff", (T.blk[:], T.blk[:], [[16, 8]], A.is_ge, 0.0, 15, -1), ["blk"], ["blk"])
+    op("g", "iota", (T.pi[:, 0:4], [[0, 4]], 0, 1), [], ["pi"])
+    op("g", "iota", (T.b16i[:], [[1, 16]], 0, 0), [], ["b16i"])
+    op("g", "aff", (T.idf[:], T.on[:], [[-1, 128]], A.is_equal, 0.0, 0, 1), ["on"], ["idf"])
+    op("g", "aff", (T.shu[:], T.on[:], [[1, 128]], A.is_equal, 0.0, -16, -1), ["on"], ["shu"])
+    op("g", "aff", (T.shd[:], T.on[:], [[1, 128]], A.is_equal, 0.0, 16, -1), ["on"], ["shd"])
+    op("g", "iota", (T.con[:, 0:64], [[0, 4], [16, 16]], 4, 0), [], ["con.o"], kw={"allow_small_or_imprecise_dtypes": True})
+    op("g", "iota", (T.con[:, 64:128], [[0, 4], [-16, 16]], 244, 0), [], ["con.c"], kw={"allow_small_or_imprecise_dtypes": True})
+    v("ms", (T.onb[:], 1.0), [], ["onb"])
+    v("cp", (T.wtf[:], T.wti[:]), ["wti"], ["wtf"])
+    for h in range(2):
+        v("cp", (T["d%d" % h][:], T.dmi[:, :, 16 * h:16 * h + 16]), ["dmi"], ["d%d" % h])
+    v("ts", (T.bw[:], T.blk[:], T.wtf[:, 0:1], 2.0, A.mult, A.mult), ["blk", "wtf"], ["bw"])
+    for q in range(8):
+        v("ts", (T.wr[:, 16 * q:16 * q + 15 * 129 + 1:129], T.onb[:, 0:16], T.bw[:, q:q + 1], None, A.mult),
+          ["onb", "bw"] + (["wr"] if q == 0 else []), ["wr.%d" % q])
+    WRK = ["wr.%d" % q for q in range(8)]
+    v("cp", (T.cf0[:], T.ci0[:]), ["ci0"], ["cf0"])
+    v("ms", (T.kc[:, 0:1], 0.0), [], ["kc0"])
+    v("cp", (T.b16[:], T.b16i[:]), ["b16i"], ["b16"])
+    v("ts", (T.pi[:, 4:8], T.pi[:, 0:4], 16, None, A.bitwise_and), ["pi"], ["pj"])
+    v("ts", (T.pi[:, 8:12], T.pi[:, 0:4], 7, None, A.bitwise_and), ["pi"], ["p7"])
+    v("ts", (T.mh[:], T.pi[:, 4:8], 0.0, None, A.is_equal), ["pj"], ["mh"])
+    v("ts", (T.mh1[:], T.mh[:], -1.0, 1.0, A.mult, A.add), ["mh"], ["mh1"])
+    for nm, src, m in (("l00", "idf", "mh"), ("l01", "shu", "mh"), ("l10", "shd", "mh1"), ("l11", "idf", "mh1")):
+        v("ts", (T[nm][:], T[src][:], T[m][:, 0:1], None, A.mult), [src, m], [nm])
+
+    def e_sum(h):
+        ep = T["cps%d" % h][:, 256:264]
+        for r in range(16):
+            op("p", "mm", (ep, T.wr[:, 128 * r:128 * r + 128], T["d%d" % h][:, r:128:16], r == 0, r == 15),
+               WRK + ["d%d" % h], ["ep%d" % h], ["cps%d" % h])
+
+    def e_fin(h):
+        v("cp", (T["ei%d" % h][:], T["cps%d" % h][:, 256:264]), ["ep%d" % h], ["ei%d" % h], ["cps%d" % h])
+        v("ts", (T["ej%d" % h][:], T["ei%d" % h][:], 2047, None, A.bitwise_and), ["ei%d" % h], ["ej%d" % h])
+        v("ts", (T["e%d" % h][:], T["ej%d" % h][:], 33.0, None, A.add), ["ej%d" % h], ["e%d" % h])
+
+    def d_rep(h, src="d"):
+        for j in range(4):
+            op("p", "mm", (T["drep%d" % h][:, :, 16 * j:16 * j + 16], T.idb[:], T["%s%d" % (src, h)][:], True, True),
+               ["idb", "%s%d" % (src, h)], ["drep%d" % h], ["drep%d" % h])
+
+    def cards(l, h, t):
+        return (T["o%d" % h][:], "o%d" % h) if l == "O" else (T["ld%d" % h][:, 192 * t:192 * t + 128], "ld%d%d" % (t, h))
+
+    def c_ps(l, h, t):
+        ap, key = cards(l, h, t)
+        c0 = 0 if l == "O" else 128
+        op("p", "mm", (T["cps%d" % h][:, c0:c0 + 128], T.idf[:], ap, True, True), ["idf", key],
+           ["cp%s%d" % (l, h)], ["cps%d" % h])
+
+    def f_pre(l, h, t):
+        ap, key = cards(l, h, t)
+        n = "fq%s%d" % (l, h)
+        v("tt", (T[n][:], T["e%d" % h][:, 0:8].indirect(T.b16[:, 0:8]), ap, A.mult), ["b16", "e%d" % h, key], [n])
+        v("ts", (T[n][:], T[n][:], 5, 4095, A.arith_shift_right, A.bitwise_and), [n], [n])
+
+    def f_add(l, h, t):
+        n = "f%s%d" % (l, h)
+        v("ts", (T[n][:], T["fq%s%d" % (l, h)][:], T.kc[:, t:t + 1], None, A.add), ["fq%s%d" % (l, h), "kc%d" % t], [n])
+
+    def gather(l, h, lo=0, hi=4):
+        for p in range(lo, hi):
+            op("s", "act", (T["x%s%d" % (l, h)][:, p, :], xtab.indirect(T["f%s%d" % (l, h)][:, 32 * p:32 * p + 32]), F.Copy),
+               XTK + ["f%s%d" % (l, h)], ["x%s%d.%d" % (l, h, p)])
+
+    def against(l, h, fn, lo=0, hi=4, step=4):
+        for p in range(lo, hi, step):
+            for bb in range(2):
+                for kq in range(4):
+                    c0 = 256 * bb + 64 * kq
+                    b0, b1 = 2 * p + bb, 2 * (p + step)
+                    v("tt", (T["mn%s%d" % (l, h)][:, b0:b1:2, 64 * kq:64 * kq + 64],
+                             T["x%s%d" % (l, h)][:, p:p + step, c0:c0 + 64],
+                             T["drep%d" % h][:, b0:b1:2, :], fn),
+                      ["x%s%d.%d" % (l, h, i) for i in range(p, p + step)] + ["drep%d" % h],
+                      ["mn%s%d.%d.%d.%d" % (l, h, i, bb, kq) for i in range(p, p + step)], ["drep%d" % h])
+
+    def mn_keys(l, h, lo, hi):
+        return ["mn%s%d.%d.%d.%d" % (l, h, i, bb, kq) for i in range(lo, hi) for bb in range(2) for kq in range(4)]
+
+    def score(l, h, c):
+        bk = "bk%s%d" % (l, h)
+        out = T[bk][:, 64 * c:64 * c + 64]
+        c0 = 0 if l == "O" else 64
+        op("p", "mm", (out, T.onb[0:1, :], T.con[0:1, c0:c0 + 64], True, False),
+           ["onb", "con.o" if l == "O" else "con.c"], ["k" + l + "%d.%d" % (h, c)], [bk])
+        K = mn_keys(l, h, 2 * c, 2 * c + 2)
+        for r in range(16):
+            op("p", "mm", (out, T.sr[:, 128 * r:128 * r + 128], T["mn%s%d" % (l, h)][:, 4 * c:4 * c + 4, r:256:16], False, r == 15),
+               SRK + K, ["k" + l + "%d.%d" % (h, c)], [bk])
+
+    def mins(l, h, step):
+        if step == 4:
+            against(l, h, A.min)
+            score(l, h, 0)
+            score(l, h, 1)
+        else:
+            for c in range(2):
+                against(l, h, A.min, 2 * c, 2 * c + 2, 2)
+                score(l, h, c)
+
+    def kkeys(l, h):
+        return ["k%s%d.0" % (l, h), "k%s%d.1" % (l, h)]
+
+    def scan(l, h):
+        if l == "O":
+            a = (T["rO%d" % h][:], T.mka[:], T["bkO%d" % h][:, 0:128], 0.0, A.add, A.min)
+        else:
+            a = (T["rC%d" % h][:], T.mkm[:, 0:128], T["bkC%d" % h][:, 0:128], 0.0, A.mult, A.max)
+        v("scan", a, kkeys(l, h) + ["mka" if l == "O" else "mkm"], ["r%s%d" % (l, h)], ["bk%s%d" % (l, h)])
+
+    def k_copy(l, h):
+        c0 = 0 if l == "O" else 128
+        op("s", "act", (T["ks%d" % h][:, c0:c0 + 128], T["bk%s%d" % (l, h)][:, 0:128], F.Copy), kkeys(l, h),
+           ["ks%d.%s" % (h, l)], ["bk%s%d" % (l, h)])
+
+    def thr(h):
+        v("ts", (T["sm%d" % h][:, 0:8], T["rO%d" % h][:, 15:128:16], 256.0, None, A.add), ["rO%d" % h], ["thr%d" % h])
+
+    def swap(h):
+        v("tt", (T["sw%d" % h][:], T["rC%d" % h][:, 15:128:16], T["sm%d" % h][:, 0:8], A.is_ge),
+          ["rC%d" % h, "thr%d" % h], ["sw%d" % h])
+
+    def count(t):
+        for h in range(2):
+            op("p", "mm", (T.cps1[:, 272:280], T.onb[:], T["sw%d" % h][:], h == 0, h == 1), ["onb", "sw%d" % h], ["cnt"], ["cps1"])
+
+    def k_fin(t):
+        c = t + 1
+        v("red", (T.kt[:, c:c + 1], T.cps1[:, 272:280], AX.X, A.add), ["cnt"], ["kt%d" % c], ["cps1"])
+        v("ts", (T.kn[:, c:c + 1], T.kt[:, c:c + 1], -15.5, 0.03125, A.add, A.mult), ["kt%d" % c], ["kn%d" % c])
+        v("ts", (T.kc[:, c:c + 1], T.kn[:, c:c + 1], -32.0, T.kt[:, c:c + 1], A.mult, A.add), ["kn%d" % c, "kt%d" % c], ["kc%d" % c])
+
+    def rest(t, h):
+        last = t == NT - 1
+        sm, si, H = T["sm%d" % h], T["si%d" % h], "%d" % h
+        cps = T["cps%d" % h]
+        v("tt", (sm[:, 8:16], T["rO" + H][:, 15:128:16], T["sw" + H][:], A.mult), ["rO" + H, "sw" + H], ["kmO" + H])
+        v("tt", (sm[:, 16:24], T["rC" + H][:, 15:128:16], T["sw" + H][:], A.mult), ["rC" + H, "sw" + H], ["kmC" + H])
+        rec = 1 <= t <= 4
+        if rec:
+            v("cp", (si[:, 0:8], T["rC" + H][:, 15:128:16]), ["rC" + H], ["ra" + H])
+        v("tt", (T["oh" + H][:], sm[:, 8:24].indirect(T.b16[:, 0:16]), T["ks" + H][:], A.is_equal),
+          ["b16", "kmO" + H, "kmC" + H, "ks" + H + ".O", "ks" + H + ".C"], ["oh" + H])
+        if rec:
+            v("ts", (si[:, 8:16], si[:, 0:8], 240, None, A.bitwise_and), ["ra" + H], ["rb" + H])
+        v("tt", (T["sel" + H][:], T["oh" + H][:], cps[:, 0:256], A.mult), ["oh" + H, "cpO" + H, "cpC" + H], ["sel" + H], ["cps" + H])
+        if rec:
+            v("ts", (sm[:, 56:64], si[:, 8:16], 256.0, 1.0, A.mult, A.add), ["rb" + H], ["rc" + H])
+        v("scan", (T["rs" + H][:], T.mkm[:], T["sel" + H][:], 0.0, A.mult, A.add), ["mkm", "sel" + H], ["rs" + H])
+        if rec:
+            v("tt", (sm[:, 64:72], sm[:, 56:64], T["sw" + H][:], A.mult), ["rc" + H, "sw" + H], ["rd" + H])
+        oj, ck = T["rs" + H][:, 15:128:16], T["rs" + H][:, 143:256:16]
+        v("tt", (sm[:, 24:32], ck, oj, A.subtract), ["rs" + H], ["dlO" + H])
+        v("tt", (sm[:, 32:40], oj, ck, A.subtract), ["rs" + H], ["dlC" + H])
+        v("tt", (T["tz" + H][:], sm[:, 24:40].indirect(T.b16[:, 0:16]), T["oh" + H][:], A.mult),
+          ["b16", "dlO" + H, "dlC" + H, "oh" + H], ["tz" + H])
+        lk, l0 = "ld%d%d" % (t, h), 192 * t
+        if rec:
+            c0 = l0 + 128 + 16 * (t - 1)
+            v("tt", (T["ld" + H][:, c0:c0 + 8], sm[:, 64:72], ck, A.add), ["rd" + H, "rs" + H], [lk + "r.a%d" % t])
+            v("tt", (T["ld" + H][:, c0 + 8:c0 + 16], sm[:, 64:72], oj, A.add), ["rd" + H, "rs" + H], [lk + "r.b%d" % t])
+        cout = T["ywC" + H][:] if last else T["ld" + H][:, l0:l0 + 128]
+        oout = T["ywO" + H][:] if last else T["o" + H][:]
+        v("tt", (cout, T["tz" + H][:, 128:256], cps[:, 128:256], A.add), ["tz" + H, "cpC" + H],
+          ["ywC" + H if last else lk], ["cps" + H])
+        if not last:
+            keys = [lk, lk + "r"] + [lk + "r.%s%d" % (c, t) for c in "ab"]
+            w = 128 + 16 * t
+
+            def send():
+                sync("g", keys, [])
+                g.remote_dma(T["ld" + H][:, l0 + 192:l0 + 192 + w], T["ld" + H][:, l0:l0 + w], T.sem["ar%d%d" % (t + 1, h)], T.sem.sent, pid, rid, mask)
+            later("g", send)
+        v("tt", (si[:, 16:24], ck, T["e" + H][:, 0:8], A.mult), ["rs" + H, "e" + H], ["q1" + H])
+        v("tt", (oout, T["tz" + H][:, 0:128], cps[:, 0:128], A.add), ["tz" + H, "cpO" + H],
+          ["ywO" + H if last else "o" + H], ["cps" + H])
+        if not last:
+            c_ps("O", h, t)
+        v("ts", (si[:, 24:32], si[:, 16:24], 5, 4095, A.arith_shift_right, A.bitwise_and), ["q1" + H], ["q2" + H])
+        v("ts", (sm[:, 40:48], si[:, 24:32], T.kc[:, t:t + 1], -float(ZC), A.add, A.add), ["q2" + H, "kc%d" % t], ["q3" + H])
+        v("tt", (sm[:, 48:56], sm[:, 40:48], T["sw" + H][:], A.mult), ["q3" + H, "sw" + H], ["q4" + H])
+        v("ts", (T["xo" + H][:], sm[:, 48:56], float(ZC), None, A.add), ["q4" + H], ["xo" + H])
+        v("tt", (T["u" + H][:], xtab.indirect(T["xo" + H][:, 0:8]), T["d" + H][:], A.is_ge), XTK + ["xo" + H, "d" + H], ["u" + H])
+        op("p", "mm", (cps[:, 384:512], T.idb[:], T["d" + H][:], True, False), ["idb", "d" + H], ["dp" + H], ["cps" + H])
+        op("p", "mm", (cps[:, 384:512], T.idn[:], T["u" + H][:], False, True), ["idn", "u" + H], ["dp" + H], ["cps" + H])
+        if last:
+            v("ts", (T.yd_s[:, :, 16 * h:16 * h + 16], cps[:, 384:512], 1.0, None, A.max), ["dp" + H], ["yd." + H], ["cps" + H])
+            return
+        v("ts", (T["d" + H][:], cps[:, 384:512], 1.0, None, A.max), ["dp" + H], ["d" + H], ["cps" + H])
+        e_sum(h)
+        if t + 1 < 4:
+            d_rep(h)
+
+    def next_pool(t, h):
+        e_fin(h)
+        f_pre("O", h, t)
+
+    def arrive(t, h):
+        sem = "ar%d%d" % (t, h)
+
+        def landed():
+            S[sem] = T.sem[sem]
+            last_w["ld%d%d" % (t, h)] = (sem, nin)
+            last_w["ld%d%dr" % (t, h)] = (sem, nin)
+        later("x", landed)
+        c_ps("C", h, t)
+        f_pre("C", h, t)
+
+    def slots(t, h):
+        H, L = "%d" % h, T["ld%d" % h]
+        rk = "ld%d%dr" % (t, h)
+        c0 = 192 * t + 128 + 16 * (t - 4)
+        def s(i):
+            return L[:, c0 + 8 * i:c0 + 8 * i + 8]
+        ne, vv = T["ne" + H], T["vv" + H]
+        def n(i):
+            return ne[:, 8 * i:8 * i + 8]
+        v("ts", (T["gg" + H][:], L[:, c0:c0 + 48], 0.5, None, A.is_ge), [rk], ["gg" + H])
+        v("ts", (T["ai" + H][:], L[:, c0:c0 + 48], -1.0, None, A.add), [rk], ["ai" + H])
+        pairs = {"p": (3, 0), "u": (5, 0), "v": (5, 2), "P": (2, 1), "U": (4, 1), "W": (4, 3)}
+        pos = {}
+        for i, (nm, (a, b)) in enumerate(pairs.items()):
+            v("tt", (n(i), s(a), s(b), A.not_equal), [rk], ["ne%s%d" % (H, i)])
+            pos[nm] = i
+        v("ts", (T["ai" + H][:], T["ai" + H][:], 4095, None, A.bitwise_and), ["ai" + H], ["ai" + H])
+        v("tt", (n(6), s(3), s(0), A.is_equal), [rk], ["ne%s6" % H])
+        v("tt", (n(7), s(2), s(1), A.is_equal), [rk], ["ne%s7" % H])
+        def k(i):
+            return "ne%s%d" % (H, i)
+        v("tt", (n(6), n(6), n(pos["W"]), A.max), [k(6), k(pos["W"])], [k(6)])
+        v("tt", (n(7), n(7), n(pos["v"]), A.max), [k(7), k(pos["v"])], [k(7)])
+        for i, (a, b) in enumerate(((pos["p"], pos["u"]), (pos["P"], pos["U"]), (pos["P"], pos["v"]),
+                                    (pos["p"], pos["W"]), (pos["U"], 6), (pos["u"], 7))):
+            v("tt", (vv[:, 8 * i:8 * i + 8], n(a), n(b), A.mult), [k(a), k(b)], ["vv%s%d" % (H, i)])
+        v("tt", (T["aq" + H][:], T["e" + H][:, 0:8].indirect(T.b8[:, 0:3]), T["ai" + H][:], A.mult),
+          ["b8", "e" + H, "ai" + H], ["aq" + H])
+        v("tt", (vv[:], vv[:], T["gg" + H][:], A.mult), ["vv%s%d" % (H, i) for i in range(6)] + ["gg" + H],
+          ["vv" + H] + ["vv%s%d" % (H, i) for i in range(6)])
+        v("ts", (T["aq" + H][:], T["aq" + H][:], 5, 4095, A.arith_shift_right, A.bitwise_and), ["aq" + H], ["aq" + H])
+
+    def slots_k(t, h):
+        H = "%d" % h
+        v("ts", (T["sf" + H][:], T["aq" + H][:], T.kc[:, t:t + 1], -float(ZC), A.add, A.add), ["aq" + H, "kc%d" % t], ["sf" + H])
+        v("tt", (T["sf" + H][:], T["sf" + H][:], T["vv" + H][:], A.mult), ["sf" + H, "vv" + H], ["sf" + H])
+        v("ts", (T["so" + H][:], T["sf" + H][:], float(ZC), None, A.add), ["sf" + H], ["so" + H])
+        op("s", "act", (T["yg" + H][:], xtab.indirect(T["so" + H][:, 0:48]), F.Copy), XTK + ["so" + H], ["yg" + H])
+
+    def step2a(h):
+        H = "%d" % h
+        y, bb, xg = T["yg" + H], T["bb" + H], T["xgi" + H]
+        v("tt", (bb[:, :, :], y[:, 0:128], y[:, 256:384], A.max), ["yg" + H], ["bb" + H])
+        v("tt", (bb[:, :, :], bb[:, :, :], y[:, 512:640], A.max), ["bb" + H, "yg" + H], ["bb" + H])
+        d_rep(h, "bb")
+        for i in range(3):
+            v("tt", (xg[:, i, :, :], y[:, 256 * i + 128:256 * i + 256], bb[:, :, :], A.is_ge), ["bb" + H, "yg" + H], ["xg%s%d" % (H, i)])
+        against("C", h, A.is_ge)
+        out = T["bkC" + H][:, 0:128]
+        for i in range(3):
+            op("p", "mm", (out, T.idm[:], xg[:, i, :, :], i == 0, False), ["idm", "xg%s%d" % (H, i)], kkeys("C", h), ["bkC" + H])
+        for k in range(16):
+            op("p", "mm", (out, T.idb[:], T["mnC" + H][:, 0:8, 16 * k:16 * k + 16], False, k == 15),
+               ["idb"] + ["mnC%s.%d.%d.%d" % (H, p, q, k // 4) for p in range(4) for q in range(2)], kkeys("C", h), ["bkC" + H])
+
+    def step2b(h):
+        H = "%d" % h
+        u, d = T["up" + H], T["d" + H]
+        U = ["up" + H]
+        v("ts", (u[:, :, :], T["bkC" + H][:, 0:128], 0.5, 16.0, A.is_ge, A.mult), kkeys("C", h), U, ["bkC" + H])
+        v("tt", (u[:, :, :], u[:, :, :], d[:], A.add), U + ["d" + H], U)
+        v("ts", (u[:, :, :], u[:, :, :], -8.0, 1.0, A.add, A.max), U, U)
+        v("ts", (d[:], u[:, :, :], 255.0, None, A.min), U, ["d" + H])
+        d_rep(h)
+
+    def turn(i, srckey, T_in, dest):
+        tt = T["tt%d" % i]
+        for b in range(8):
+            v("tr", (tt[:, b, :], T_in(b)), srckey, ["tt%d.%d" % (i, b)])
+        K = ["tt%d.%d" % (i, b) for b in range(8)]
+        for q in range(2):
+            bk = "bk%s%d" % ("OC"[i], q)
+            for s_ in range(2):
+                op("p", "mm", (T[bk][:, 0:128], T["l%d%d" % (q, s_)][:], tt[:, :, 16 * s_:16 * s_ + 16], s_ == 0, s_ == 1),
+                   ["l%d%d" % (q, s_)] + K, kkeys("OC"[i], q), [bk])
+            out, keys = dest(q)
+            op("s", "act", (out, T[bk][:, 0:128], F.Copy), kkeys("OC"[i], q), keys, [bk])
+
+    def turn_out(l, h):
+        tt, K = T["tt%d" % (l == "C")], ["to%s%d.%d" % (l, h, b) for b in range(4)]
+        for b in range(4):
+            v("tr", (tt[:, 4 * h + b, :], T["yw%s%d" % (l, h)][:, 32 * b:32 * b + 32]), ["yw%s%d" % (l, h)], [K[b]])
+        bk = "bk%s%d" % (l, h)
+        for q in range(2):
+            out = T[bk][:, 64 * q:64 * q + 64]
+            for s_ in range(2):
+                op("p", "mm", (out, T["l%d%d" % (q, s_)][:], tt[:, 4 * h:4 * h + 4, 16 * s_:16 * s_ + 16], s_ == 0, s_ == 1),
+                   ["l%d%d" % (q, s_)] + K, ["k%s%d.%d" % (l, h, q)], [bk])
+        for q in range(2):
+            op("s", "act", (T["y" + l][:, q:8:2, 16 * h:16 * h + 16], T[bk][:, 64 * q:64 * q + 64], F.Copy),
+               ["k%s%d.%d" % (l, h, q)], ["y%s%d%d" % (l, h, q)], [bk])
+
+    SRK = ["sr.%d" % q for q in range(8)]
+    e_sum(0)
+    e_sum(1)
+    turn(0, ["cf0"], lambda b: T.cf0[:, 32 * b:32 * b + 32], lambda q: (T["o%d" % q][:], ["o%d" % q]))
+    v("ms", (T.xt_s[:, ZC:ZC + 16], -1.0), [], ["xt.z"])
+    v("ts", (T.bs[:], T.blk[:], 512.0, None, A.mult), ["blk"], ["bs"])
+    v("ms", (T.sr[:], 0.0), [], ["sr"])
+    v("cp", (T.cf1[:], T.ci1[:]), ["ci1"], ["cf1"])
+    turn(1, ["cf1"], lambda b: T.cf1[:, 32 * b:32 * b + 32], lambda q: (T["ld%d" % q][:, 0:128], ["ld0%d" % q]))
+    for q in range(8):
+        op("s", "act", (T.sr[:, 16 * q:16 * q + 15 * 129 + 1:129], T.onb[:, 0:16], F.Copy, 0.0, T.bs[:, q:q + 1]),
+           ["onb", "bs"] + (["sr"] if q == 0 else []), ["sr.%d" % q])
+    v("cp", (T.idb[:], T.idf[:]), ["idf"], ["idb"])
+    next_pool(0, 0)
+    f_add("O", 0, 0)
+    gather("O", 0)
+    for h in range(2):
+        d_rep(h)
+        c_ps("O", h, 0)
+        c_ps("C", h, 0)
+    f_pre("C", 0, 0)
+    f_add("C", 0, 0)
+    gather("C", 0)
+    next_pool(0, 1)
+    f_add("O", 1, 0)
+    gather("O", 1)
+    v("ms", (T.mkm[:], 1.0), [], ["mkm"])
+    v("ms", (T.mka[:], 0.0), [], ["mka"])
+    v("ms", (T.mkm[:, 0:256:16], 0.0), [], ["mkm"])
+    v("ms", (T.mka[:, 0:128:16], 8388608.0), [], ["mka"])
+    v("ts", (T.idn[:], T.idb[:], -4.0, None, A.mult), ["idb"], ["idn"])
+    v("ts", (T.idm[:], T.idb[:], -1.0, None, A.mult), ["idb"], ["idm"])
+    v("cp", (T.b8[:], T.pi[:, 8:12]), ["p7"], ["b8"])
+    f_pre("C", 1, 0)
+    f_add("C", 1, 0)
+
+    R = []
+    for t in range(NT):
+        two, more = t >= 4, t < NT - 1
+        kch = []
+        if t > 0:
+            kch = seq((k_fin, t - 1), (f_add, "C" if two else "O", 0, t), (gather, "C" if two else "O", 0))
+        r1, R = split(R, 3)
+        run(r1)
+        run(kch)
+        n1 = seq((next_pool, t - 1, 1), (f_add, "O", 1, t)) if t > 0 else []
+        if not two:
+            if t > 0:
+                a0 = seq((arrive, t, 0), (f_add, "C", 0, t))
+                r0, R = split(R, 4)
+                r1, R = split(R, 6)
+                run(r0)
+                weave(a0, r1)
+                gather("C", 0)
+            run(R)
+            run(seq((mins, "O", 0, 2)))
+            m0, m1 = split(seq((mins, "C", 0, 2)), 8)
+            weave(n1, m0)
+            if t > 0:
+                gather("O", 1)
+            weave(m1, seq((scan, "O", 0), (thr, 0)))
+            k_copy("O", 0)
+            m0, m1 = split(seq((mins, "O", 1, 2)), LEAD)
+            weave(seq((arrive, t, 1), (f_add, "C", 1, t)) if t > 0 else [], m0)
+            run(seq((scan, "C", 0), (swap, 0), (k_copy, "C", 0), (gather, "C", 1)))
+            weave(seq((rest, t, 0)), m1)
+            c0, c1 = split(seq((mins, "C", 1, 2)), 8)
+            run(c0)
+            ra, rb = split(seq((next_pool, t, 0), (scan, "O", 1), (thr, 1)), 7)
+            weave(ra, c1)
+            c1 = []
+        else:
+            weave(seq((slots_k, t, 0), (f_add, "O", 0, t)), R)
+            sa, sb = split(seq((step2a, 0)), 2)
+            run(sa)
+            gather("O", 0)
+            weave(sb, n1)
+            run(seq((arrive, t, 1), (f_add, "C", 1, t), (gather, "C", 1)))
+            sa, sb = split(seq((step2b, 0)), 3)
+            weave(seq((slots, t, 1)), sa)
+            weave(seq((slots_k, t, 1)), sb)
+            run(seq((mins, "C", 0, 4), (mins, "O", 0, 4)))
+            k_copy("C", 0)
+            sa, sb = split(seq((step2a, 1)), 5)
+            run(seq((scan, "C", 0)))
+            run(sa)
+            run(seq((scan, "O", 0), (k_copy, "O", 0), (thr, 0), (swap, 0)))
+            ra, rb = split(seq((rest, t, 0)), 10)
+            run(sb)
+            gather("O", 1)
+            run(ra)
+            m0, m1 = split(seq((step2b, 1), (mins, "O", 1, 2), (mins, "C", 1, 2)), 4 + 16)
+            weave(rb, m0)
+            c0, c1 = split(m1, 8)
+            run(c0)
+            x0 = seq((scan, "O", 1), (thr, 1))
+            if not more:
+                x0 = seq((turn_out, "C", 0), (turn_out, "O", 0)) + x0
+            weave(x0, c1)
+            c1 = []
+        if more:
+            if two:
+                run(seq((next_pool, t, 0)))
+            if t + 1 >= 4:
+                run(seq((arrive, t + 1, 0), (slots, t + 1, 0)))
+        k_copy("O", 1)
+        scan("C", 1)
+        swap(1)
+        k_copy("C", 1)
+        if more:
+            count(t)
+        R = seq((rest, t, 1))
+
+    r0, R = split(R, 9)
+    run(r0)
+    r1, R = split(R, 6)
+    weave(seq((turn_out, "C", 1)), r1)
+    weave(seq((turn_out, "O", 1)), R)
+    for l, y, sem in (("C", T.yc, "oc"), ("O", T.yo, "oo")):
+        sync("y", ["y%s%d%d" % (l, h, q) for h in range(2) for q in range(2)], [])
+        g.sync.dma_start(y[:], T["y" + l][:]).then_inc(T.sem[sem], 16)
+    sync("s", ["yd.0", "yd.1"], [])
+    g.scalar.dma_start(T.yd[:], T.yd_s[:]).then_inc(T.sem.od, 16)
+    for q in "vspg":
+        g.wait_ge(S[q], cnt[q])
+    g.wait_ge(T.sem.sent, nout * 2 * (NT - 1))
+    for sem in ("lxt", "lwr", "lwt", "ldm", "lpo", "lpk", "oc", "oo", "od"):
+        g.wait_ge(T.sem[sem], 16)
+    for t in range(1, NT):
+        for h in range(2):
+            g.wait_ge(T.sem["ar%d%d" % (t, h)], nin)

@@ -3,7 +3,11 @@ from concourse.mybir import AluOpType as A, ActivationFunctionType as F, AxisLis
 W = 4096
 ZC = 4128
 NT = 6
-LEAD = 8
+NR, NM = 3, 6
+NK, NW, N1 = 3, 2, 2
+LC = 8
+GV = 2
+LEAD = 6
 SCRATCH = {
     "xt_s": ("sbuf", [128, 4144], "bfloat16"),
     "wti": ("sbuf", [128, 1], "int32"), "wtf": ("sbuf", [128, 1], "float32"),
@@ -35,7 +39,6 @@ for _h in "01":
         "o" + _h: ("sbuf", [128, 128], "float32"),
         "d" + _h: ("sbuf", [128, 128], "bfloat16"),
         "e" + _h: ("sbuf", [128, 8], "float32"), "ei" + _h: ("sbuf", [128, 8], "int32"),
-        "ej" + _h: ("sbuf", [128, 8], "int32"),
         "drep" + _h: ("psum", [128, 8, 64], "float32"),
         "bkO" + _h: ("psum", [128, 512], "float32"), "bkC" + _h: ("psum", [128, 512], "float32"),
         "cps" + _h: ("psum", [128, 512], "float32"),
@@ -48,7 +51,8 @@ for _h in "01":
         "xo" + _h: ("sbuf", [128, 8], "uint16"),
         "u" + _h: ("sbuf", [128, 128], "bfloat16"),
         "aq" + _h: ("sbuf", [128, 48], "int32"),
-        "ai" + _h: ("sbuf", [128, 48], "int32"), "vv" + _h: ("sbuf", [128, 48], "float32"),
+        "ai" + _h: ("sbuf", [128, 48], "int32"), "vv" + _h: ("sbuf", [128, 3, 16], "float32"),
+        "rb" + _h: ("sbuf", [128, 3, 16], "float32"),
         "gg" + _h: ("sbuf", [128, 48], "float32"), "ne" + _h: ("sbuf", [128, 64], "float32"),
         "so" + _h: ("sbuf", [128, 48], "uint16"), "sf" + _h: ("sbuf", [128, 48], "float32"),
         "yg" + _h: ("sbuf", [128, 768], "bfloat16"), "xgi" + _h: ("sbuf", [128, 3, 8, 16], "bfloat16"),
@@ -149,6 +153,10 @@ def rank_program(g, core, T, topo):
                     return L[:i], L[i:]
         return L, []
 
+    def till_sent(L):
+        i = [z[0] for z in L].index("g") + 1 if "g" in [z[0] for z in L] else 0
+        return L[:i], L[i:]
+
     def weave(*Ls):
         items = []
         for j, L in enumerate(Ls):
@@ -229,8 +237,8 @@ def rank_program(g, core, T, topo):
 
     def e_fin(h):
         v("cp", (T["ei%d" % h][:], T["cps%d" % h][:, 256:264]), ["ep%d" % h], ["ei%d" % h], ["cps%d" % h])
-        v("ts", (T["ej%d" % h][:], T["ei%d" % h][:], 2047, None, A.bitwise_and), ["ei%d" % h], ["ej%d" % h])
-        v("ts", (T["e%d" % h][:], T["ej%d" % h][:], 33.0, None, A.add), ["ej%d" % h], ["e%d" % h])
+        v("ts", (T["ei%d" % h][:], T["ei%d" % h][:], 2047, None, A.bitwise_and), ["ei%d" % h], ["ei%d" % h])
+        v("ts", (T["e%d" % h][:], T["ei%d" % h][:], 33.0, None, A.add), ["ei%d" % h], ["e%d" % h])
 
     def d_rep(h, src="d"):
         for j in range(4):
@@ -294,7 +302,7 @@ def rank_program(g, core, T, topo):
             score(l, h, 1)
         else:
             for c in range(2):
-                against(l, h, A.min, 2 * c, 2 * c + 2, 2)
+                against(l, h, A.min, 2 * c, 2 * c + 2, step if c else 2)
                 score(l, h, c)
 
     def kkeys(l, h):
@@ -349,36 +357,42 @@ def rank_program(g, core, T, topo):
         if rec:
             v("tt", (sm[:, 64:72], sm[:, 56:64], T["sw" + H][:], A.mult), ["rc" + H, "sw" + H], ["rd" + H])
         oj, ck = T["rs" + H][:, 15:128:16], T["rs" + H][:, 143:256:16]
-        v("tt", (sm[:, 24:32], ck, oj, A.subtract), ["rs" + H], ["dlO" + H])
-        v("tt", (sm[:, 32:40], oj, ck, A.subtract), ["rs" + H], ["dlC" + H])
-        v("tt", (T["tz" + H][:], sm[:, 24:40].indirect(T.b16[:, 0:16]), T["oh" + H][:], A.mult),
-          ["b16", "dlO" + H, "dlC" + H, "oh" + H], ["tz" + H])
         lk, l0 = "ld%d%d" % (t, h), 192 * t
-        if rec:
-            c0 = l0 + 128 + 16 * (t - 1)
-            v("tt", (T["ld" + H][:, c0:c0 + 8], sm[:, 64:72], ck, A.add), ["rd" + H, "rs" + H], [lk + "r.a%d" % t])
-            v("tt", (T["ld" + H][:, c0 + 8:c0 + 16], sm[:, 64:72], oj, A.add), ["rd" + H, "rs" + H], [lk + "r.b%d" % t])
-        cout = T["ywC" + H][:] if last else T["ld" + H][:, l0:l0 + 128]
-        oout = T["ywO" + H][:] if last else T["o" + H][:]
-        v("tt", (cout, T["tz" + H][:, 128:256], cps[:, 128:256], A.add), ["tz" + H, "cpC" + H],
-          ["ywC" + H if last else lk], ["cps" + H])
-        if not last:
-            keys = [lk, lk + "r"] + [lk + "r.%s%d" % (c, t) for c in "ab"]
-            w = 128 + 16 * t
 
-            def send():
-                sync("g", keys, [])
-                g.remote_dma(T["ld" + H][:, l0 + 192:l0 + 192 + w], T["ld" + H][:, l0:l0 + w], T.sem["ar%d%d" % (t + 1, h)], T.sem.sent, pid, rid, mask)
-            later("g", send)
-        v("tt", (si[:, 16:24], ck, T["e" + H][:, 0:8], A.mult), ["rs" + H, "e" + H], ["q1" + H])
-        v("tt", (oout, T["tz" + H][:, 0:128], cps[:, 0:128], A.add), ["tz" + H, "cpO" + H],
-          ["ywO" + H if last else "o" + H], ["cps" + H])
-        if not last:
-            c_ps("O", h, t)
-        v("ts", (si[:, 24:32], si[:, 16:24], 5, 4095, A.arith_shift_right, A.bitwise_and), ["q1" + H], ["q2" + H])
-        v("ts", (sm[:, 40:48], si[:, 24:32], T.kc[:, t:t + 1], -float(ZC), A.add, A.add), ["q2" + H, "kc%d" % t], ["q3" + H])
-        v("tt", (sm[:, 48:56], sm[:, 40:48], T["sw" + H][:], A.mult), ["q3" + H, "sw" + H], ["q4" + H])
-        v("ts", (T["xo" + H][:], sm[:, 48:56], float(ZC), None, A.add), ["q4" + H], ["xo" + H])
+        def send():
+            w = 128 + 16 * t
+            sync("g", [lk, lk + "r"] + [lk + "r.%s%d" % (c, t) for c in "ab"], [])
+            g.remote_dma(T["ld" + H][:, l0 + 192:l0 + 192 + w], T["ld" + H][:, l0:l0 + w], T.sem["ar%d%d" % (t + 1, h)],
+                         T.sem.sent, pid, rid, mask)
+
+        def exchange():
+            v("tt", (sm[:, 24:32], ck, oj, A.subtract), ["rs" + H], ["dlO" + H])
+            v("tt", (sm[:, 32:40], oj, ck, A.subtract), ["rs" + H], ["dlC" + H])
+            if rec:
+                c0 = l0 + 128 + 16 * (t - 1)
+                v("tt", (T["ld" + H][:, c0:c0 + 8], sm[:, 64:72], ck, A.add), ["rd" + H, "rs" + H], [lk + "r.a%d" % t])
+                v("tt", (T["ld" + H][:, c0 + 8:c0 + 16], sm[:, 64:72], oj, A.add), ["rd" + H, "rs" + H], [lk + "r.b%d" % t])
+            v("tt", (T["tz" + H][:], sm[:, 24:40].indirect(T.b16[:, 0:16]), T["oh" + H][:], A.mult),
+              ["b16", "dlO" + H, "dlC" + H, "oh" + H], ["tz" + H])
+            cout = T["ywC" + H][:] if last else T["ld" + H][:, l0:l0 + 128]
+            oout = T["ywO" + H][:] if last else T["o" + H][:]
+            v("tt", (cout, T["tz" + H][:, 128:256], cps[:, 128:256], A.add), ["tz" + H, "cpC" + H],
+              ["ywC" + H if last else lk], ["cps" + H])
+            if not last:
+                later("g", send)
+            v("tt", (oout, T["tz" + H][:, 0:128], cps[:, 0:128], A.add), ["tz" + H, "cpO" + H],
+              ["ywO" + H if last else "o" + H], ["cps" + H])
+            if not last and h:
+                c_ps("O", h, t)
+
+        exch = seq((exchange,))
+        dem = seq((v, "tt", (si[:, 16:24], ck, T["e" + H][:, 0:8], A.mult), ["rs" + H, "e" + H], ["q1" + H]),
+                  (v, "ts", (sm[:, 40:48], T["sw" + H][:], -8192.0, 8192.0, A.mult, A.add), ["sw" + H], ["pen" + H]),
+                  (v, "ts", (si[:, 24:32], si[:, 16:24], 5, 4095, A.arith_shift_right, A.bitwise_and), ["q1" + H], ["q2" + H]),
+                  (v, "tt", (sm[:, 48:56], si[:, 24:32], sm[:, 40:48], A.add), ["q2" + H, "pen" + H], ["q3" + H]),
+                  (v, "ts", (T["xo" + H][:], sm[:, 48:56], T.kc[:, t:t + 1], float(ZC), A.add, A.min),
+                   ["q3" + H, "kc%d" % t], ["xo" + H]))
+        weave(exch, dem)
         v("tt", (T["u" + H][:], xtab.indirect(T["xo" + H][:, 0:8]), T["d" + H][:], A.is_ge), XTK + ["xo" + H, "d" + H], ["u" + H])
         op("p", "mm", (cps[:, 384:512], T.idb[:], T["d" + H][:], True, False), ["idb", "d" + H], ["dp" + H], ["cps" + H])
         op("p", "mm", (cps[:, 384:512], T.idn[:], T["u" + H][:], False, True), ["idn", "u" + H], ["dp" + H], ["cps" + H])
@@ -387,7 +401,7 @@ def rank_program(g, core, T, topo):
             return
         v("ts", (T["d" + H][:], cps[:, 384:512], 1.0, None, A.max), ["dp" + H], ["d" + H], ["cps" + H])
         e_sum(h)
-        if t + 1 < 4:
+        if t + 1 < 4 and h:
             d_rep(h)
 
     def next_pool(t, h):
@@ -405,42 +419,42 @@ def rank_program(g, core, T, topo):
         c_ps("C", h, t)
         f_pre("C", h, t)
 
+    def slots_in(t, h):
+        L, rk, c0 = T["ld%d" % h], ["ld%d%dr" % (t, h)], 192 * t + 128 + 16 * (t - 4)
+        v("cp", (T["rb%d" % h][:, :, :], L[:, c0:c0 + 48]), rk, ["rb%d" % h])
+        v("ts", (T["gg%d" % h][:], L[:, c0:c0 + 48], 0.5, None, A.is_ge), rk, ["gg%d" % h])
+
     def slots(t, h):
         H, L = "%d" % h, T["ld%d" % h]
         rk = "ld%d%dr" % (t, h)
         c0 = 192 * t + 128 + 16 * (t - 4)
-        def s(i):
-            return L[:, c0 + 8 * i:c0 + 8 * i + 8]
-        ne, vv = T["ne" + H], T["vv" + H]
-        def n(i):
-            return ne[:, 8 * i:8 * i + 8]
-        v("ts", (T["gg" + H][:], L[:, c0:c0 + 48], 0.5, None, A.is_ge), [rk], ["gg" + H])
+        rb, ne, vv = T["rb" + H], T["ne" + H], T["vv" + H]
+        def k(*i):
+            return ["ne%s%d" % (H, j) for j in i]
+        def n(i, j):
+            return ne[:, 8 * i:8 * j]
         v("ts", (T["ai" + H][:], L[:, c0:c0 + 48], -1.0, None, A.add), [rk], ["ai" + H])
-        pairs = {"p": (3, 0), "u": (5, 0), "v": (5, 2), "P": (2, 1), "U": (4, 1), "W": (4, 3)}
-        pos = {}
-        for i, (nm, (a, b)) in enumerate(pairs.items()):
-            v("tt", (n(i), s(a), s(b), A.not_equal), [rk], ["ne%s%d" % (H, i)])
-            pos[nm] = i
+        v("tt", (n(1, 3), rb[:, 1:3, 8:16], rb[:, 0:2, 0:8], A.not_equal), ["rb" + H], k(1, 2))
+        v("tt", (n(4, 6), rb[:, 1:3, 0:8], rb[:, 0:2, 8:16], A.not_equal), ["rb" + H], k(4, 5))
         v("ts", (T["ai" + H][:], T["ai" + H][:], 4095, None, A.bitwise_and), ["ai" + H], ["ai" + H])
-        v("tt", (n(6), s(3), s(0), A.is_equal), [rk], ["ne%s6" % H])
-        v("tt", (n(7), s(2), s(1), A.is_equal), [rk], ["ne%s7" % H])
-        def k(i):
-            return "ne%s%d" % (H, i)
-        v("tt", (n(6), n(6), n(pos["W"]), A.max), [k(6), k(pos["W"])], [k(6)])
-        v("tt", (n(7), n(7), n(pos["v"]), A.max), [k(7), k(pos["v"])], [k(7)])
-        for i, (a, b) in enumerate(((pos["p"], pos["u"]), (pos["P"], pos["U"]), (pos["P"], pos["v"]),
-                                    (pos["p"], pos["W"]), (pos["U"], 6), (pos["u"], 7))):
-            v("tt", (vv[:, 8 * i:8 * i + 8], n(a), n(b), A.mult), [k(a), k(b)], ["vv%s%d" % (H, i)])
+        v("tt", (n(0, 1), rb[:, 2, 0:8], rb[:, 0, 8:16], A.not_equal), ["rb" + H], k(0))
+        v("tt", (n(3, 4), rb[:, 2, 8:16], rb[:, 0, 0:8], A.not_equal), ["rb" + H], k(3))
+        v("tt", (n(6, 7), n(5, 6), n(1, 2), A.is_ge), k(5, 1), k(6))
+        v("tt", (n(7, 8), n(2, 3), n(4, 5), A.is_ge), k(2, 4), k(7))
+        v("tt", (vv[:, 0:2, 8:16], n(4, 6), n(0, 2), A.mult), k(4, 5, 0, 1), ["vv%s0" % H])
+        v("tt", (vv[:, 0:2, 0:8], n(1, 3), n(3, 5), A.mult), k(1, 2, 3, 4), ["vv%s1" % H])
+        v("tt", (vv[:, 2, 0:8], n(0, 1), n(6, 7), A.mult), k(0, 6), ["vv%s2" % H])
+        v("tt", (vv[:, 2, 8:16], n(3, 4), n(7, 8), A.mult), k(3, 7), ["vv%s3" % H])
         v("tt", (T["aq" + H][:], T["e" + H][:, 0:8].indirect(T.b8[:, 0:3]), T["ai" + H][:], A.mult),
           ["b8", "e" + H, "ai" + H], ["aq" + H])
-        v("tt", (vv[:], vv[:], T["gg" + H][:], A.mult), ["vv%s%d" % (H, i) for i in range(6)] + ["gg" + H],
-          ["vv" + H] + ["vv%s%d" % (H, i) for i in range(6)])
+        VV = ["vv%s%d" % (H, i) for i in range(4)]
+        v("tt", (vv[:, :, :], vv[:, :, :], T["gg" + H][:], A.mult), VV + ["gg" + H], ["vv" + H] + VV)
         v("ts", (T["aq" + H][:], T["aq" + H][:], 5, 4095, A.arith_shift_right, A.bitwise_and), ["aq" + H], ["aq" + H])
 
     def slots_k(t, h):
         H = "%d" % h
         v("ts", (T["sf" + H][:], T["aq" + H][:], T.kc[:, t:t + 1], -float(ZC), A.add, A.add), ["aq" + H, "kc%d" % t], ["sf" + H])
-        v("tt", (T["sf" + H][:], T["sf" + H][:], T["vv" + H][:], A.mult), ["sf" + H, "vv" + H], ["sf" + H])
+        v("tt", (T["sf" + H][:], T["sf" + H][:], T["vv" + H][:, :, :], A.mult), ["sf" + H, "vv" + H], ["sf" + H])
         v("ts", (T["so" + H][:], T["sf" + H][:], float(ZC), None, A.add), ["sf" + H], ["so" + H])
         op("s", "act", (T["yg" + H][:], xtab.indirect(T["so" + H][:, 0:48]), F.Copy), XTK + ["so" + H], ["yg" + H])
 
@@ -450,9 +464,10 @@ def rank_program(g, core, T, topo):
         v("tt", (bb[:, :, :], y[:, 0:128], y[:, 256:384], A.max), ["yg" + H], ["bb" + H])
         v("tt", (bb[:, :, :], bb[:, :, :], y[:, 512:640], A.max), ["bb" + H, "yg" + H], ["bb" + H])
         d_rep(h, "bb")
+        against("C", h, A.is_ge, 0, 4, 2)
         for i in range(3):
-            v("tt", (xg[:, i, :, :], y[:, 256 * i + 128:256 * i + 256], bb[:, :, :], A.is_ge), ["bb" + H, "yg" + H], ["xg%s%d" % (H, i)])
-        against("C", h, A.is_ge)
+            v("tt", (xg[:, i, :, :], y[:, 256 * i + 128:256 * i + 256], T["drep" + H][:, :, 0:16], A.is_ge),
+              ["drep" + H, "yg" + H], ["xg%s%d" % (H, i)], ["drep" + H])
         out = T["bkC" + H][:, 0:128]
         for i in range(3):
             op("p", "mm", (out, T.idm[:], xg[:, i, :, :], i == 0, False), ["idm", "xg%s%d" % (H, i)], kkeys("C", h), ["bkC" + H])
@@ -513,14 +528,15 @@ def rank_program(g, core, T, topo):
     next_pool(0, 0)
     f_add("O", 0, 0)
     gather("O", 0)
+    e_fin(1)
     for h in range(2):
         d_rep(h)
         c_ps("O", h, 0)
         c_ps("C", h, 0)
     f_pre("C", 0, 0)
     f_add("C", 0, 0)
-    gather("C", 0)
-    next_pool(0, 1)
+    gather("C", 0, 0, 4 - GV)
+    f_pre("O", 1, 0)
     f_add("O", 1, 0)
     gather("O", 1)
     v("ms", (T.mkm[:], 1.0), [], ["mkm"])
@@ -532,6 +548,8 @@ def rank_program(g, core, T, topo):
     v("cp", (T.b8[:], T.pi[:, 8:12]), ["p7"], ["b8"])
     f_pre("C", 1, 0)
     f_add("C", 1, 0)
+    for p in range(4 - GV, 4):
+        v("cp", (T.xC0[:, p, :], xtab.indirect(T.fC0[:, 32 * p:32 * p + 32])), XTK + ["fC0"], ["xC0.%d" % p])
 
     R = []
     for t in range(NT):
@@ -539,20 +557,25 @@ def rank_program(g, core, T, topo):
         kch = []
         if t > 0:
             kch = seq((k_fin, t - 1), (f_add, "C" if two else "O", 0, t), (gather, "C" if two else "O", 0))
-        r1, R = split(R, 3)
+        r1, R = split(R, NK)
         run(r1)
-        run(kch)
+        if two:
+            run(seq((arrive, t, 0), (slots_in, t, 0)))
+        r1, R = split(R, NW)
+        weave(kch, r1)
         n1 = seq((next_pool, t - 1, 1), (f_add, "O", 1, t)) if t > 0 else []
+        if t > 0 and not two:
+            r0, R = split(R, N1)
+            run(r0)
+            r1, R = split(R, 3)
+            weave(seq((arrive, t, 0), (f_add, "C", 0, t)), r1)
+            gather("C", 0)
         if not two:
-            if t > 0:
-                a0 = seq((arrive, t, 0), (f_add, "C", 0, t))
-                r0, R = split(R, 4)
-                r1, R = split(R, 6)
-                run(r0)
-                weave(a0, r1)
-                gather("C", 0)
-            run(R)
-            run(seq((mins, "O", 0, 2)))
+            r0, R = split(R, NR)
+            run(r0)
+            m0, m1 = split(seq((mins, "O", 0, 2)), NM)
+            weave(R, m0)
+            run(m1)
             m0, m1 = split(seq((mins, "C", 0, 2)), 8)
             weave(n1, m0)
             if t > 0:
@@ -565,56 +588,51 @@ def rank_program(g, core, T, topo):
             weave(seq((rest, t, 0)), m1)
             c0, c1 = split(seq((mins, "C", 1, 2)), 8)
             run(c0)
-            ra, rb = split(seq((next_pool, t, 0), (scan, "O", 1), (thr, 1)), 7)
-            weave(ra, c1)
-            c1 = []
+            m0, m1 = split(c1, LC)
+            run(m0)
+            weave(seq((next_pool, t, 0)), seq((scan, "O", 1), (thr, 1)), m1)
         else:
-            weave(seq((slots_k, t, 0), (f_add, "O", 0, t)), R)
+            weave(seq((slots, t, 0), (slots_k, t, 0), (f_add, "O", 0, t)), R)
+            gather("O", 0)
             sa, sb = split(seq((step2a, 0)), 2)
             run(sa)
-            gather("O", 0)
-            weave(sb, n1)
-            run(seq((arrive, t, 1), (f_add, "C", 1, t), (gather, "C", 1)))
-            sa, sb = split(seq((step2b, 0)), 3)
-            weave(seq((slots, t, 1)), sa)
-            weave(seq((slots_k, t, 1)), sb)
-            run(seq((mins, "C", 0, 4), (mins, "O", 0, 4)))
-            k_copy("C", 0)
-            sa, sb = split(seq((step2a, 1)), 5)
-            run(seq((scan, "C", 0)))
+            run(n1)
+            run(sb)
+            run(seq((arrive, t, 1), (slots_in, t, 1), (f_add, "C", 1, t), (gather, "C", 1)))
+            run(seq((slots, t, 1)))
+            weave(seq((slots_k, t, 1)), seq((step2b, 0)))
+            m0, m1 = split(seq((mins, "C", 0, 4)), 4)
+            run(m0 + m1)
+            sa, sb = split(seq((step2a, 1)), 2)
             run(sa)
+            run(seq((mins, "O", 0, 4)))
+            run(seq((scan, "C", 0), (k_copy, "C", 0)))
+            run(sb)
             run(seq((scan, "O", 0), (k_copy, "O", 0), (thr, 0), (swap, 0)))
             ra, rb = split(seq((rest, t, 0)), 10)
-            run(sb)
             gather("O", 1)
             run(ra)
             m0, m1 = split(seq((step2b, 1), (mins, "O", 1, 2), (mins, "C", 1, 2)), 4 + 16)
             weave(rb, m0)
             c0, c1 = split(m1, 8)
-            run(c0)
-            x0 = seq((scan, "O", 1), (thr, 1))
-            if not more:
-                x0 = seq((turn_out, "C", 0), (turn_out, "O", 0)) + x0
-            weave(x0, c1)
-            c1 = []
-        if more:
-            if two:
+            run(c0 + c1)
+            run(seq((scan, "O", 1), (thr, 1)))
+            if more:
                 run(seq((next_pool, t, 0)))
-            if t + 1 >= 4:
-                run(seq((arrive, t + 1, 0), (slots, t + 1, 0)))
         k_copy("O", 1)
         scan("C", 1)
         swap(1)
         k_copy("C", 1)
         if more:
             count(t)
+            c_ps("O", 0, t)
+            if t + 1 < 4:
+                d_rep(0)
         R = seq((rest, t, 1))
 
-    r0, R = split(R, 9)
-    run(r0)
-    r1, R = split(R, 6)
-    weave(seq((turn_out, "C", 1)), r1)
-    weave(seq((turn_out, "O", 1)), R)
+    r0, R = split(R, 15)
+    weave(r0, seq((turn_out, "C", 0), (turn_out, "O", 0)))
+    weave(seq((turn_out, "C", 1), (turn_out, "O", 1)), R)
     for l, y, sem in (("C", T.yc, "oc"), ("O", T.yo, "oo")):
         sync("y", ["y%s%d%d" % (l, h, q) for h in range(2) for q in range(2)], [])
         g.sync.dma_start(y[:], T["y" + l][:]).then_inc(T.sem[sem], 16)

from concourse.mybir import AluOpType as A, ActivationFunctionType as F, AxisListType as AX

W = 4096
ZC = 4128
NT = 6
NR, NM = 3, 6
NK, NW, N1 = 3, 2, 2
LC = 8
GV = 2
LEAD = 6
SCRATCH = {
    "xt_s": ("sbuf", [128, 4144], "bfloat16"),
    "wti": ("sbuf", [128, 1], "int32"), "wtf": ("sbuf", [128, 1], "float32"),
    "dmi": ("sbuf", [128, 8, 32], "int32"),
    "ci0": ("sbuf", [128, 256], "int32"), "ci1": ("sbuf", [128, 256], "int32"),
    "cf0": ("sbuf", [128, 256], "float32"), "cf1": ("sbuf", [128, 256], "float32"),
    "tt0": ("sbuf", [128, 8, 32], "float32"), "tt1": ("sbuf", [128, 8, 32], "float32"),
    "ywO0": ("sbuf", [128, 128], "float32"), "ywC0": ("sbuf", [128, 128], "float32"),
    "ywO1": ("sbuf", [128, 128], "float32"), "ywC1": ("sbuf", [128, 128], "float32"),
    "yO": ("sbuf", [128, 8, 32], "float32"), "yC": ("sbuf", [128, 8, 32], "float32"),
    "yd_s": ("sbuf", [128, 8, 32], "float32"),
    "on": ("sbuf", [128, 128], "float32"), "onb": ("sbuf", [128, 128], "bfloat16"),
    "idf": ("sbuf", [128, 128], "float32"), "idb": ("sbuf", [128, 128], "bfloat16"),
    "idn": ("sbuf", [128, 128], "bfloat16"), "idm": ("sbuf", [128, 128], "bfloat16"),
    "shu": ("sbuf", [128, 128], "float32"), "shd": ("sbuf", [128, 128], "float32"),
    "l00": ("sbuf", [128, 128], "float32"), "l01": ("sbuf", [128, 128], "float32"),
    "l10": ("sbuf", [128, 128], "float32"), "l11": ("sbuf", [128, 128], "float32"),
    "blk": ("sbuf", [128, 8], "float32"), "bs": ("sbuf", [128, 8], "float32"), "bw": ("sbuf", [128, 8], "float32"),
    "pi": ("sbuf", [128, 12], "int32"),
    "mh": ("sbuf", [128, 4], "float32"), "mh1": ("sbuf", [128, 4], "float32"),
    "b16i": ("sbuf", [128, 16], "int32"), "b16": ("sbuf", [128, 16], "uint16"), "b8": ("sbuf", [128, 4], "uint16"),
    "con": ("sbuf", [128, 128], "bfloat16"),
    "sr": ("sbuf", [128, 2048], "bfloat16"), "wr": ("sbuf", [128, 2048], "bfloat16"),
    "mkm": ("sbuf", [128, 256], "float32"), "mka": ("sbuf", [128, 128], "float32"),
    "kc": ("sbuf", [128, 8], "float32"), "kn": ("sbuf", [128, 8], "int32"), "kt": ("sbuf", [128, 8], "float32"),
}
for _h in "01":
    SCRATCH.update({
        "o" + _h: ("sbuf", [128, 128], "float32"),
        "d" + _h: ("sbuf", [128, 128], "bfloat16"),
        "e" + _h: ("sbuf", [128, 8], "float32"), "ei" + _h: ("sbuf", [128, 8], "int32"),
        "drep" + _h: ("psum", [128, 8, 64], "float32"),
        "bkO" + _h: ("psum", [128, 512], "float32"), "bkC" + _h: ("psum", [128, 512], "float32"),
        "cps" + _h: ("psum", [128, 512], "float32"),
        "ks" + _h: ("sbuf", [128, 256], "float32"),
        "oh" + _h: ("sbuf", [128, 256], "float32"), "sel" + _h: ("sbuf", [128, 256], "float32"),
        "rs" + _h: ("sbuf", [128, 256], "float32"), "tz" + _h: ("sbuf", [128, 256], "float32"),
        "sm" + _h: ("sbuf", [128, 80], "float32"),
        "si" + _h: ("sbuf", [128, 32], "int32"),
        "sw" + _h: ("sbuf", [128, 8], "bfloat16"),
        "xo" + _h: ("sbuf", [128, 8], "uint16"),
        "u" + _h: ("sbuf", [128, 128], "bfloat16"),
        "aq" + _h: ("sbuf", [128, 48], "int32"),
        "ai" + _h: ("sbuf", [128, 48], "int32"), "vv" + _h: ("sbuf", [128, 3, 16], "float32"),
        "rb" + _h: ("sbuf", [128, 3, 16], "float32"),
        "gg" + _h: ("sbuf", [128, 48], "float32"), "ne" + _h: ("sbuf", [128, 64], "float32"),
        "so" + _h: ("sbuf", [128, 48], "uint16"), "sf" + _h: ("sbuf", [128, 48], "float32"),
        "yg" + _h: ("sbuf", [128, 768], "bfloat16"), "xgi" + _h: ("sbuf", [128, 3, 8, 16], "bfloat16"),
        "bb" + _h: ("sbuf", [128, 8, 16], "bfloat16"), "up" + _h: ("sbuf", [128, 8, 16], "float32"),
    })
    for _l in "OC":
        SCRATCH.update({
            "fq" + _l + _h: ("sbuf", [128, 128], "int32"), "f" + _l + _h: ("sbuf", [128, 128], "uint16"),
            "x" + _l + _h: ("sbuf", [128, 4, 512], "bfloat16"), "mn" + _l + _h: ("sbuf", [128, 8, 256], "bfloat16"),
            "r" + _l + _h: ("sbuf", [128, 128], "float32"),
        })
    SCRATCH["ld" + _h] = ("sbuf", [128, 192 * NT], "float32")
SEMAPHORES = (["sv", "ss", "sp", "sg", "sent", "lxt", "lwr", "lwt", "ldm", "lpo", "lpk", "oc", "oo", "od"]
              + ["ar%d%d" % (t, h) for t in range(1, NT) for h in range(2)])


def rank_program(g, core, T, topo):
    rank = T.rank_of(core)
    if rank is None:
        return
    nxt = T.cores[(rank + 1) % len(T.cores)]
    prv = T.cores[(rank - 1) % len(T.cores)]
    rid, pid = topo.addr(nxt)[0], topo.addr(nxt)[1]
    mask = topo.mask(core, nxt)
    nout, nin = len(topo.engines(core, nxt)), len(topo.engines(prv, core))
    Q = {"v": g.vector, "s": g.scalar, "p": g.tensor, "g": g, "y": g.sync}
    S = {"v": T.sem.sv, "s": T.sem.ss, "p": T.sem.sp, "g": T.sem.sg}
    cnt = {q: 0 for q in Q}
    known = {q: {} for q in Q}
    clk, last_w, reads, banks = {}, {}, {}, {}

    def need(q, dep):
        q2, n = dep
        if known[q].get(q2, 0) >= n:
            return
        Q[q].wait_ge(S[q2], n)
        known[q][q2] = n
        for a, m in clk.get(dep, {}).items():
            if known[q].get(a, 0) < m:
                known[q][a] = m

    def sync(q, R, Wr, B=()):
        deps = {}
        def add(d):
            if q == "p" and d[0] == "p":
                return
            deps[d[0]] = max(deps.get(d[0], 0), d[1])
        for k in R:
            if k in last_w:
                add(last_w[k])
        for k in Wr:
            if k in last_w:
                add(last_w[k])
            for d in reads.get(k, {}).items():
                add(d)
        for b in B:
            for d in banks.get(b, {}).items():
                if d[0] != q:
                    add(d)
        for d in sorted(deps.items(), key=lambda z: (z[0] == q, z[0])):
            need(q, d)

    def note(q, n, R, Wr, B=()):
        for k in R:
            reads.setdefault(k, {})[q] = n
        for k in Wr:
            last_w[k] = (q, n)
            reads[k] = {}
        for b in B:
            banks.setdefault(b, {})[q] = n
        clk[(q, n)] = dict(known[q])

    buf = [None]

    def later(q, fn):
        if buf[0] is None:
            fn()
        else:
            buf[0].append((q, fn))

    def seq(*fns):
        old, buf[0] = buf[0], []
        for fn in fns:
            fn[0](*fn[1:])
        out, buf[0] = buf[0], old
        return out

    def run(L):
        for z in L:
            later(z[0], z[1])

    def split(L, n):
        k = 0
        for i, z in enumerate(L):
            if z[0] == "v":
                k += 1
                if k > n:
                    return L[:i], L[i:]
        return L, []

    def till_sent(L):
        i = [z[0] for z in L].index("g") + 1 if "g" in [z[0] for z in L] else 0
        return L[:i], L[i:]

    def weave(*Ls):
        items = []
        for j, L in enumerate(Ls):
            nv, k = max(1, sum(1 for z in L if z[0] == "v")), 0
            for i, z in enumerate(L):
                if z[0] == "v":
                    k += 1
                items.append(((k - 0.5) / nv if k else 0.0, j, i, z))
        run([z[3] for z in sorted(items, key=lambda z: z[:3])])

    def op(q, name, args, R, Wr, B=(), kw=None):
        later(q, lambda: op_now(q, name, args, R, Wr, B, kw))

    def op_now(q, name, args, R, Wr, B, kw):
        sync(q, R, Wr, B)
        cnt[q] += 1
        m = {"v": {"tt": g.vector.tensor_tensor, "ts": g.vector.tensor_scalar, "cp": g.vector.tensor_copy,
                   "ms": g.vector.memset, "red": g.vector.tensor_reduce, "scan": g.vector.tensor_tensor_scan,
                   "tr": g.vector.transpose},
             "s": {"act": g.scalar.activation}, "p": {"mm": g.tensor.matmul},
             "g": {"iota": g.iota, "aff": g.affine_select}}[q][name]
        m(*args, **(kw or {})).then_inc(S[q], 1)
        note(q, cnt[q], R, Wr, B)

    def v(name, args, R, Wr, B=(), **kw):
        op("v", name, args, R, Wr, B, kw)

    def load(q, sem, out, in_, keys):
        Q[q].dma_start(out, in_).then_inc(T.sem[sem], 16)
        S[sem] = T.sem[sem]
        for k in keys:
            last_w[k] = (sem, 16)

    load("y", "lwt", T.wti[:], T.wt[:], ["wti"])
    load("y", "ldm", T.dmi[:], T.dm[:], ["dmi"])
    load("s", "lxt", T.xt_s[:, 0:W], T.xt[:], ["xt.m"])
    load("y", "lpo", T.ci0[:], T.po[:], ["ci0"])
    load("y", "lpk", T.ci1[:], T.pk[:], ["ci1"])
    load("s", "lwr", T.xt_s[:, W:W + 32], T.xt[:, 0:32], ["xt.w"])
    XTK = ["xt.m", "xt.w", "xt.z"]
    xtab = T.xt_s[:, 0:4144]

    v("ms", (T.on[:], 1.0), [], ["on"])
    v("ms", (T.wr[:], 0.0), [], ["wr"])
    op("g", "aff", (T.blk[:], T.on[:, 0:8], [[-16, 8]], A.is_ge, 0.0, 0, 1), ["on"], ["blk"])
    op("g", "aff", (T.blk[:], T.blk[:], [[16, 8]], A.is_ge, 0.0, 15, -1), ["blk"], ["blk"])
    op("g", "iota", (T.pi[:, 0:4], [[0, 4]], 0, 1), [], ["pi"])
    op("g", "iota", (T.b16i[:], [[1, 16]], 0, 0), [], ["b16i"])
    op("g", "aff", (T.idf[:], T.on[:], [[-1, 128]], A.is_equal, 0.0, 0, 1), ["on"], ["idf"])
    op("g", "aff", (T.shu[:], T.on[:], [[1, 128]], A.is_equal, 0.0, -16, -1), ["on"], ["shu"])
    op("g", "aff", (T.shd[:], T.on[:], [[1, 128]], A.is_equal, 0.0, 16, -1), ["on"], ["shd"])
    op("g", "iota", (T.con[:, 0:64], [[0, 4], [16, 16]], 4, 0), [], ["con.o"], kw={"allow_small_or_imprecise_dtypes": True})
    op("g", "iota", (T.con[:, 64:128], [[0, 4], [-16, 16]], 244, 0), [], ["con.c"], kw={"allow_small_or_imprecise_dtypes": True})
    v("ms", (T.onb[:], 1.0), [], ["onb"])
    v("cp", (T.wtf[:], T.wti[:]), ["wti"], ["wtf"])
    for h in range(2):
        v("cp", (T["d%d" % h][:], T.dmi[:, :, 16 * h:16 * h + 16]), ["dmi"], ["d%d" % h])
    v("ts", (T.bw[:], T.blk[:], T.wtf[:, 0:1], 2.0, A.mult, A.mult), ["blk", "wtf"], ["bw"])
    for q in range(8):
        v("ts", (T.wr[:, 16 * q:16 * q + 15 * 129 + 1:129], T.onb[:, 0:16], T.bw[:, q:q + 1], None, A.mult),
          ["onb", "bw"] + (["wr"] if q == 0 else []), ["wr.%d" % q])
    WRK = ["wr.%d" % q for q in range(8)]
    v("cp", (T.cf0[:], T.ci0[:]), ["ci0"], ["cf0"])
    v("ms", (T.kc[:, 0:1], 0.0), [], ["kc0"])
    v("cp", (T.b16[:], T.b16i[:]), ["b16i"], ["b16"])
    v("ts", (T.pi[:, 4:8], T.pi[:, 0:4], 16, None, A.bitwise_and), ["pi"], ["pj"])
    v("ts", (T.pi[:, 8:12], T.pi[:, 0:4], 7, None, A.bitwise_and), ["pi"], ["p7"])
    v("ts", (T.mh[:], T.pi[:, 4:8], 0.0, None, A.is_equal), ["pj"], ["mh"])
    v("ts", (T.mh1[:], T.mh[:], -1.0, 1.0, A.mult, A.add), ["mh"], ["mh1"])
    for nm, src, m in (("l00", "idf", "mh"), ("l01", "shu", "mh"), ("l10", "shd", "mh1"), ("l11", "idf", "mh1")):
        v("ts", (T[nm][:], T[src][:], T[m][:, 0:1], None, A.mult), [src, m], [nm])

    def e_sum(h):
        ep = T["cps%d" % h][:, 256:264]
        for r in range(16):
            op("p", "mm", (ep, T.wr[:, 128 * r:128 * r + 128], T["d%d" % h][:, r:128:16], r == 0, r == 15),
               WRK + ["d%d" % h], ["ep%d" % h], ["cps%d" % h])

    def e_fin(h):
        v("cp", (T["ei%d" % h][:], T["cps%d" % h][:, 256:264]), ["ep%d" % h], ["ei%d" % h], ["cps%d" % h])
        v("ts", (T["ei%d" % h][:], T["ei%d" % h][:], 2047, None, A.bitwise_and), ["ei%d" % h], ["ei%d" % h])
        v("ts", (T["e%d" % h][:], T["ei%d" % h][:], 33.0, None, A.add), ["ei%d" % h], ["e%d" % h])

    def d_rep(h, src="d"):
        for j in range(4):
            op("p", "mm", (T["drep%d" % h][:, :, 16 * j:16 * j + 16], T.idb[:], T["%s%d" % (src, h)][:], True, True),
               ["idb", "%s%d" % (src, h)], ["drep%d" % h], ["drep%d" % h])

    def cards(l, h, t):
        return (T["o%d" % h][:], "o%d" % h) if l == "O" else (T["ld%d" % h][:, 192 * t:192 * t + 128], "ld%d%d" % (t, h))

    def c_ps(l, h, t):
        ap, key = cards(l, h, t)
        c0 = 0 if l == "O" else 128
        op("p", "mm", (T["cps%d" % h][:, c0:c0 + 128], T.idf[:], ap, True, True), ["idf", key],
           ["cp%s%d" % (l, h)], ["cps%d" % h])

    def f_pre(l, h, t):
        ap, key = cards(l, h, t)
        n = "fq%s%d" % (l, h)
        v("tt", (T[n][:], T["e%d" % h][:, 0:8].indirect(T.b16[:, 0:8]), ap, A.mult), ["b16", "e%d" % h, key], [n])
        v("ts", (T[n][:], T[n][:], 5, 4095, A.arith_shift_right, A.bitwise_and), [n], [n])

    def f_add(l, h, t):
        n = "f%s%d" % (l, h)
        v("ts", (T[n][:], T["fq%s%d" % (l, h)][:], T.kc[:, t:t + 1], None, A.add), ["fq%s%d" % (l, h), "kc%d" % t], [n])

    def gather(l, h, lo=0, hi=4):
        for p in range(lo, hi):
            op("s", "act", (T["x%s%d" % (l, h)][:, p, :], xtab.indirect(T["f%s%d" % (l, h)][:, 32 * p:32 * p + 32]), F.Copy),
               XTK + ["f%s%d" % (l, h)], ["x%s%d.%d" % (l, h, p)])

    def against(l, h, fn, lo=0, hi=4, step=4):
        for p in range(lo, hi, step):
            for bb in range(2):
                for kq in range(4):
                    c0 = 256 * bb + 64 * kq
                    b0, b1 = 2 * p + bb, 2 * (p + step)
                    v("tt", (T["mn%s%d" % (l, h)][:, b0:b1:2, 64 * kq:64 * kq + 64],
                             T["x%s%d" % (l, h)][:, p:p + step, c0:c0 + 64],
                             T["drep%d" % h][:, b0:b1:2, :], fn),
                      ["x%s%d.%d" % (l, h, i) for i in range(p, p + step)] + ["drep%d" % h],
                      ["mn%s%d.%d.%d.%d" % (l, h, i, bb, kq) for i in range(p, p + step)], ["drep%d" % h])

    def mn_keys(l, h, lo, hi):
        return ["mn%s%d.%d.%d.%d" % (l, h, i, bb, kq) for i in range(lo, hi) for bb in range(2) for kq in range(4)]

    def score(l, h, c):
        bk = "bk%s%d" % (l, h)
        out = T[bk][:, 64 * c:64 * c + 64]
        c0 = 0 if l == "O" else 64
        op("p", "mm", (out, T.onb[0:1, :], T.con[0:1, c0:c0 + 64], True, False),
           ["onb", "con.o" if l == "O" else "con.c"], ["k" + l + "%d.%d" % (h, c)], [bk])
        K = mn_keys(l, h, 2 * c, 2 * c + 2)
        for r in range(16):
            op("p", "mm", (out, T.sr[:, 128 * r:128 * r + 128], T["mn%s%d" % (l, h)][:, 4 * c:4 * c + 4, r:256:16], False, r == 15),
               SRK + K, ["k" + l + "%d.%d" % (h, c)], [bk])

    def mins(l, h, step):
        if step == 4:
            against(l, h, A.min)
            score(l, h, 0)
            score(l, h, 1)
        else:
            for c in range(2):
                against(l, h, A.min, 2 * c, 2 * c + 2, step if c else 2)
                score(l, h, c)

    def kkeys(l, h):
        return ["k%s%d.0" % (l, h), "k%s%d.1" % (l, h)]

    def scan(l, h):
        if l == "O":
            a = (T["rO%d" % h][:], T.mka[:], T["bkO%d" % h][:, 0:128], 0.0, A.add, A.min)
        else:
            a = (T["rC%d" % h][:], T.mkm[:, 0:128], T["bkC%d" % h][:, 0:128], 0.0, A.mult, A.max)
        v("scan", a, kkeys(l, h) + ["mka" if l == "O" else "mkm"], ["r%s%d" % (l, h)], ["bk%s%d" % (l, h)])

    def k_copy(l, h):
        c0 = 0 if l == "O" else 128
        op("s", "act", (T["ks%d" % h][:, c0:c0 + 128], T["bk%s%d" % (l, h)][:, 0:128], F.Copy), kkeys(l, h),
           ["ks%d.%s" % (h, l)], ["bk%s%d" % (l, h)])

    def thr(h):
        v("ts", (T["sm%d" % h][:, 0:8], T["rO%d" % h][:, 15:128:16], 256.0, None, A.add), ["rO%d" % h], ["thr%d" % h])

    def swap(h):
        v("tt", (T["sw%d" % h][:], T["rC%d" % h][:, 15:128:16], T["sm%d" % h][:, 0:8], A.is_ge),
          ["rC%d" % h, "thr%d" % h], ["sw%d" % h])

    def count(t):
        for h in range(2):
            op("p", "mm", (T.cps1[:, 272:280], T.onb[:], T["sw%d" % h][:], h == 0, h == 1), ["onb", "sw%d" % h], ["cnt"], ["cps1"])

    def k_fin(t):
        c = t + 1
        v("red", (T.kt[:, c:c + 1], T.cps1[:, 272:280], AX.X, A.add), ["cnt"], ["kt%d" % c], ["cps1"])
        v("ts", (T.kn[:, c:c + 1], T.kt[:, c:c + 1], -15.5, 0.03125, A.add, A.mult), ["kt%d" % c], ["kn%d" % c])
        v("ts", (T.kc[:, c:c + 1], T.kn[:, c:c + 1], -32.0, T.kt[:, c:c + 1], A.mult, A.add), ["kn%d" % c, "kt%d" % c], ["kc%d" % c])

    def rest(t, h):
        last = t == NT - 1
        sm, si, H = T["sm%d" % h], T["si%d" % h], "%d" % h
        cps = T["cps%d" % h]
        v("tt", (sm[:, 8:16], T["rO" + H][:, 15:128:16], T["sw" + H][:], A.mult), ["rO" + H, "sw" + H], ["kmO" + H])
        v("tt", (sm[:, 16:24], T["rC" + H][:, 15:128:16], T["sw" + H][:], A.mult), ["rC" + H, "sw" + H], ["kmC" + H])
        rec = 1 <= t <= 4
        if rec:
            v("cp", (si[:, 0:8], T["rC" + H][:, 15:128:16]), ["rC" + H], ["ra" + H])
        v("tt", (T["oh" + H][:], sm[:, 8:24].indirect(T.b16[:, 0:16]), T["ks" + H][:], A.is_equal),
          ["b16", "kmO" + H, "kmC" + H, "ks" + H + ".O", "ks" + H + ".C"], ["oh" + H])
        if rec:
            v("ts", (si[:, 8:16], si[:, 0:8], 240, None, A.bitwise_and), ["ra" + H], ["rb" + H])
        v("tt", (T["sel" + H][:], T["oh" + H][:], cps[:, 0:256], A.mult), ["oh" + H, "cpO" + H, "cpC" + H], ["sel" + H], ["cps" + H])
        if rec:
            v("ts", (sm[:, 56:64], si[:, 8:16], 256.0, 1.0, A.mult, A.add), ["rb" + H], ["rc" + H])
        v("scan", (T["rs" + H][:], T.mkm[:], T["sel" + H][:], 0.0, A.mult, A.add), ["mkm", "sel" + H], ["rs" + H])
        if rec:
            v("tt", (sm[:, 64:72], sm[:, 56:64], T["sw" + H][:], A.mult), ["rc" + H, "sw" + H], ["rd" + H])
        oj, ck = T["rs" + H][:, 15:128:16], T["rs" + H][:, 143:256:16]
        lk, l0 = "ld%d%d" % (t, h), 192 * t

        def send():
            w = 128 + 16 * t
            sync("g", [lk, lk + "r"] + [lk + "r.%s%d" % (c, t) for c in "ab"], [])
            g.remote_dma(T["ld" + H][:, l0 + 192:l0 + 192 + w], T["ld" + H][:, l0:l0 + w], T.sem["ar%d%d" % (t + 1, h)],
                         T.sem.sent, pid, rid, mask)

        def exchange():
            v("tt", (sm[:, 24:32], ck, oj, A.subtract), ["rs" + H], ["dlO" + H])
            v("tt", (sm[:, 32:40], oj, ck, A.subtract), ["rs" + H], ["dlC" + H])
            if rec:
                c0 = l0 + 128 + 16 * (t - 1)
                v("tt", (T["ld" + H][:, c0:c0 + 8], sm[:, 64:72], ck, A.add), ["rd" + H, "rs" + H], [lk + "r.a%d" % t])
                v("tt", (T["ld" + H][:, c0 + 8:c0 + 16], sm[:, 64:72], oj, A.add), ["rd" + H, "rs" + H], [lk + "r.b%d" % t])
            v("tt", (T["tz" + H][:], sm[:, 24:40].indirect(T.b16[:, 0:16]), T["oh" + H][:], A.mult),
              ["b16", "dlO" + H, "dlC" + H, "oh" + H], ["tz" + H])
            cout = T["ywC" + H][:] if last else T["ld" + H][:, l0:l0 + 128]
            oout = T["ywO" + H][:] if last else T["o" + H][:]
            v("tt", (cout, T["tz" + H][:, 128:256], cps[:, 128:256], A.add), ["tz" + H, "cpC" + H],
              ["ywC" + H if last else lk], ["cps" + H])
            if not last:
                later("g", send)
            v("tt", (oout, T["tz" + H][:, 0:128], cps[:, 0:128], A.add), ["tz" + H, "cpO" + H],
              ["ywO" + H if last else "o" + H], ["cps" + H])
            if not last and h:
                c_ps("O", h, t)

        exch = seq((exchange,))
        dem = seq((v, "tt", (si[:, 16:24], ck, T["e" + H][:, 0:8], A.mult), ["rs" + H, "e" + H], ["q1" + H]),
                  (v, "ts", (sm[:, 40:48], T["sw" + H][:], -8192.0, 8192.0, A.mult, A.add), ["sw" + H], ["pen" + H]),
                  (v, "ts", (si[:, 24:32], si[:, 16:24], 5, 4095, A.arith_shift_right, A.bitwise_and), ["q1" + H], ["q2" + H]),
                  (v, "tt", (sm[:, 48:56], si[:, 24:32], sm[:, 40:48], A.add), ["q2" + H, "pen" + H], ["q3" + H]),
                  (v, "ts", (T["xo" + H][:], sm[:, 48:56], T.kc[:, t:t + 1], float(ZC), A.add, A.min),
                   ["q3" + H, "kc%d" % t], ["xo" + H]))
        weave(exch, dem)
        v("tt", (T["u" + H][:], xtab.indirect(T["xo" + H][:, 0:8]), T["d" + H][:], A.is_ge), XTK + ["xo" + H, "d" + H], ["u" + H])
        op("p", "mm", (cps[:, 384:512], T.idb[:], T["d" + H][:], True, False), ["idb", "d" + H], ["dp" + H], ["cps" + H])
        op("p", "mm", (cps[:, 384:512], T.idn[:], T["u" + H][:], False, True), ["idn", "u" + H], ["dp" + H], ["cps" + H])
        if last:
            v("ts", (T.yd_s[:, :, 16 * h:16 * h + 16], cps[:, 384:512], 1.0, None, A.max), ["dp" + H], ["yd." + H], ["cps" + H])
            return
        v("ts", (T["d" + H][:], cps[:, 384:512], 1.0, None, A.max), ["dp" + H], ["d" + H], ["cps" + H])
        e_sum(h)
        if t + 1 < 4 and h:
            d_rep(h)

    def next_pool(t, h):
        e_fin(h)
        f_pre("O", h, t)

    def arrive(t, h):
        sem = "ar%d%d" % (t, h)

        def landed():
            S[sem] = T.sem[sem]
            last_w["ld%d%d" % (t, h)] = (sem, nin)
            last_w["ld%d%dr" % (t, h)] = (sem, nin)
        later("x", landed)
        c_ps("C", h, t)
        f_pre("C", h, t)

    def slots_in(t, h):
        L, rk, c0 = T["ld%d" % h], ["ld%d%dr" % (t, h)], 192 * t + 128 + 16 * (t - 4)
        v("cp", (T["rb%d" % h][:, :, :], L[:, c0:c0 + 48]), rk, ["rb%d" % h])
        v("ts", (T["gg%d" % h][:], L[:, c0:c0 + 48], 0.5, None, A.is_ge), rk, ["gg%d" % h])

    def slots(t, h):
        H, L = "%d" % h, T["ld%d" % h]
        rk = "ld%d%dr" % (t, h)
        c0 = 192 * t + 128 + 16 * (t - 4)
        rb, ne, vv = T["rb" + H], T["ne" + H], T["vv" + H]
        def k(*i):
            return ["ne%s%d" % (H, j) for j in i]
        def n(i, j):
            return ne[:, 8 * i:8 * j]
        v("ts", (T["ai" + H][:], L[:, c0:c0 + 48], -1.0, None, A.add), [rk], ["ai" + H])
        v("tt", (n(1, 3), rb[:, 1:3, 8:16], rb[:, 0:2, 0:8], A.not_equal), ["rb" + H], k(1, 2))
        v("tt", (n(4, 6), rb[:, 1:3, 0:8], rb[:, 0:2, 8:16], A.not_equal), ["rb" + H], k(4, 5))
        v("ts", (T["ai" + H][:], T["ai" + H][:], 4095, None, A.bitwise_and), ["ai" + H], ["ai" + H])
        v("tt", (n(0, 1), rb[:, 2, 0:8], rb[:, 0, 8:16], A.not_equal), ["rb" + H], k(0))
        v("tt", (n(3, 4), rb[:, 2, 8:16], rb[:, 0, 0:8], A.not_equal), ["rb" + H], k(3))
        v("tt", (n(6, 7), n(5, 6), n(1, 2), A.is_ge), k(5, 1), k(6))
        v("tt", (n(7, 8), n(2, 3), n(4, 5), A.is_ge), k(2, 4), k(7))
        v("tt", (vv[:, 0:2, 8:16], n(4, 6), n(0, 2), A.mult), k(4, 5, 0, 1), ["vv%s0" % H])
        v("tt", (vv[:, 0:2, 0:8], n(1, 3), n(3, 5), A.mult), k(1, 2, 3, 4), ["vv%s1" % H])
        v("tt", (vv[:, 2, 0:8], n(0, 1), n(6, 7), A.mult), k(0, 6), ["vv%s2" % H])
        v("tt", (vv[:, 2, 8:16], n(3, 4), n(7, 8), A.mult), k(3, 7), ["vv%s3" % H])
        v("tt", (T["aq" + H][:], T["e" + H][:, 0:8].indirect(T.b8[:, 0:3]), T["ai" + H][:], A.mult),
          ["b8", "e" + H, "ai" + H], ["aq" + H])
        VV = ["vv%s%d" % (H, i) for i in range(4)]
        v("tt", (vv[:, :, :], vv[:, :, :], T["gg" + H][:], A.mult), VV + ["gg" + H], ["vv" + H] + VV)
        v("ts", (T["aq" + H][:], T["aq" + H][:], 5, 4095, A.arith_shift_right, A.bitwise_and), ["aq" + H], ["aq" + H])

    def slots_k(t, h):
        H = "%d" % h
        v("ts", (T["sf" + H][:], T["aq" + H][:], T.kc[:, t:t + 1], -float(ZC), A.add, A.add), ["aq" + H, "kc%d" % t], ["sf" + H])
        v("tt", (T["sf" + H][:], T["sf" + H][:], T["vv" + H][:, :, :], A.mult), ["sf" + H, "vv" + H], ["sf" + H])
        v("ts", (T["so" + H][:], T["sf" + H][:], float(ZC), None, A.add), ["sf" + H], ["so" + H])
        op("s", "act", (T["yg" + H][:], xtab.indirect(T["so" + H][:, 0:48]), F.Copy), XTK + ["so" + H], ["yg" + H])

    def step2a(h):
        H = "%d" % h
        y, bb, xg = T["yg" + H], T["bb" + H], T["xgi" + H]
        v("tt", (bb[:, :, :], y[:, 0:128], y[:, 256:384], A.max), ["yg" + H], ["bb" + H])
        v("tt", (bb[:, :, :], bb[:, :, :], y[:, 512:640], A.max), ["bb" + H, "yg" + H], ["bb" + H])
        d_rep(h, "bb")
        against("C", h, A.is_ge, 0, 4, 2)
        for i in range(3):
            v("tt", (xg[:, i, :, :], y[:, 256 * i + 128:256 * i + 256], T["drep" + H][:, :, 0:16], A.is_ge),
              ["drep" + H, "yg" + H], ["xg%s%d" % (H, i)], ["drep" + H])
        out = T["bkC" + H][:, 0:128]
        for i in range(3):
            op("p", "mm", (out, T.idm[:], xg[:, i, :, :], i == 0, False), ["idm", "xg%s%d" % (H, i)], kkeys("C", h), ["bkC" + H])
        for k in range(16):
            op("p", "mm", (out, T.idb[:], T["mnC" + H][:, 0:8, 16 * k:16 * k + 16], False, k == 15),
               ["idb"] + ["mnC%s.%d.%d.%d" % (H, p, q, k // 4) for p in range(4) for q in range(2)], kkeys("C", h), ["bkC" + H])

    def step2b(h):
        H = "%d" % h
        u, d = T["up" + H], T["d" + H]
        U = ["up" + H]
        v("ts", (u[:, :, :], T["bkC" + H][:, 0:128], 0.5, 16.0, A.is_ge, A.mult), kkeys("C", h), U, ["bkC" + H])
        v("tt", (u[:, :, :], u[:, :, :], d[:], A.add), U + ["d" + H], U)
        v("ts", (u[:, :, :], u[:, :, :], -8.0, 1.0, A.add, A.max), U, U)
        v("ts", (d[:], u[:, :, :], 255.0, None, A.min), U, ["d" + H])
        d_rep(h)

    def turn(i, srckey, T_in, dest):
        tt = T["tt%d" % i]
        for b in range(8):
            v("tr", (tt[:, b, :], T_in(b)), srckey, ["tt%d.%d" % (i, b)])
        K = ["tt%d.%d" % (i, b) for b in range(8)]
        for q in range(2):
            bk = "bk%s%d" % ("OC"[i], q)
            for s_ in range(2):
                op("p", "mm", (T[bk][:, 0:128], T["l%d%d" % (q, s_)][:], tt[:, :, 16 * s_:16 * s_ + 16], s_ == 0, s_ == 1),
                   ["l%d%d" % (q, s_)] + K, kkeys("OC"[i], q), [bk])
            out, keys = dest(q)
            op("s", "act", (out, T[bk][:, 0:128], F.Copy), kkeys("OC"[i], q), keys, [bk])

    def turn_out(l, h):
        tt, K = T["tt%d" % (l == "C")], ["to%s%d.%d" % (l, h, b) for b in range(4)]
        for b in range(4):
            v("tr", (tt[:, 4 * h + b, :], T["yw%s%d" % (l, h)][:, 32 * b:32 * b + 32]), ["yw%s%d" % (l, h)], [K[b]])
        bk = "bk%s%d" % (l, h)
        for q in range(2):
            out = T[bk][:, 64 * q:64 * q + 64]
            for s_ in range(2):
                op("p", "mm", (out, T["l%d%d" % (q, s_)][:], tt[:, 4 * h:4 * h + 4, 16 * s_:16 * s_ + 16], s_ == 0, s_ == 1),
                   ["l%d%d" % (q, s_)] + K, ["k%s%d.%d" % (l, h, q)], [bk])
        for q in range(2):
            op("s", "act", (T["y" + l][:, q:8:2, 16 * h:16 * h + 16], T[bk][:, 64 * q:64 * q + 64], F.Copy),
               ["k%s%d.%d" % (l, h, q)], ["y%s%d%d" % (l, h, q)], [bk])

    SRK = ["sr.%d" % q for q in range(8)]
    e_sum(0)
    e_sum(1)
    turn(0, ["cf0"], lambda b: T.cf0[:, 32 * b:32 * b + 32], lambda q: (T["o%d" % q][:], ["o%d" % q]))
    v("ms", (T.xt_s[:, ZC:ZC + 16], -1.0), [], ["xt.z"])
    v("ts", (T.bs[:], T.blk[:], 512.0, None, A.mult), ["blk"], ["bs"])
    v("ms", (T.sr[:], 0.0), [], ["sr"])
    v("cp", (T.cf1[:], T.ci1[:]), ["ci1"], ["cf1"])
    turn(1, ["cf1"], lambda b: T.cf1[:, 32 * b:32 * b + 32], lambda q: (T["ld%d" % q][:, 0:128], ["ld0%d" % q]))
    for q in range(8):
        op("s", "act", (T.sr[:, 16 * q:16 * q + 15 * 129 + 1:129], T.onb[:, 0:16], F.Copy, 0.0, T.bs[:, q:q + 1]),
           ["onb", "bs"] + (["sr"] if q == 0 else []), ["sr.%d" % q])
    v("cp", (T.idb[:], T.idf[:]), ["idf"], ["idb"])
    next_pool(0, 0)
    f_add("O", 0, 0)
    gather("O", 0)
    e_fin(1)
    for h in range(2):
        d_rep(h)
        c_ps("O", h, 0)
        c_ps("C", h, 0)
    f_pre("C", 0, 0)
    f_add("C", 0, 0)
    gather("C", 0, 0, 4 - GV)
    f_pre("O", 1, 0)
    f_add("O", 1, 0)
    gather("O", 1)
    v("ms", (T.mkm[:], 1.0), [], ["mkm"])
    v("ms", (T.mka[:], 0.0), [], ["mka"])
    v("ms", (T.mkm[:, 0:256:16], 0.0), [], ["mkm"])
    v("ms", (T.mka[:, 0:128:16], 8388608.0), [], ["mka"])
    v("ts", (T.idn[:], T.idb[:], -4.0, None, A.mult), ["idb"], ["idn"])
    v("ts", (T.idm[:], T.idb[:], -1.0, None, A.mult), ["idb"], ["idm"])
    v("cp", (T.b8[:], T.pi[:, 8:12]), ["p7"], ["b8"])
    f_pre("C", 1, 0)
    f_add("C", 1, 0)
    for p in range(4 - GV, 4):
        v("cp", (T.xC0[:, p, :], xtab.indirect(T.fC0[:, 32 * p:32 * p + 32])), XTK + ["fC0"], ["xC0.%d" % p])

    R = []
    for t in range(NT):
        two, more = t >= 4, t < NT - 1
        kch = []
        if t > 0:
            kch = seq((k_fin, t - 1), (f_add, "C" if two else "O", 0, t), (gather, "C" if two else "O", 0))
        r1, R = split(R, NK)
        run(r1)
        if two:
            run(seq((arrive, t, 0), (slots_in, t, 0)))
        r1, R = split(R, NW)
        weave(kch, r1)
        n1 = seq((next_pool, t - 1, 1), (f_add, "O", 1, t)) if t > 0 else []
        if t > 0 and not two:
            r0, R = split(R, N1)
            run(r0)
            r1, R = split(R, 3)
            weave(seq((arrive, t, 0), (f_add, "C", 0, t)), r1)
            gather("C", 0)
        if not two:
            r0, R = split(R, NR)
            run(r0)
            m0, m1 = split(seq((mins, "O", 0, 2)), NM)
            weave(R, m0)
            run(m1)
            m0, m1 = split(seq((mins, "C", 0, 2)), 8)
            weave(n1, m0)
            if t > 0:
                gather("O", 1)
            weave(m1, seq((scan, "O", 0), (thr, 0)))
            k_copy("O", 0)
            m0, m1 = split(seq((mins, "O", 1, 2)), LEAD)
            weave(seq((arrive, t, 1), (f_add, "C", 1, t)) if t > 0 else [], m0)
            run(seq((scan, "C", 0), (swap, 0), (k_copy, "C", 0), (gather, "C", 1)))
            weave(seq((rest, t, 0)), m1)
            c0, c1 = split(seq((mins, "C", 1, 2)), 8)
            run(c0)
            m0, m1 = split(c1, LC)
            run(m0)
            weave(seq((next_pool, t, 0)), seq((scan, "O", 1), (thr, 1)), m1)
        else:
            weave(seq((slots, t, 0), (slots_k, t, 0), (f_add, "O", 0, t)), R)
            gather("O", 0)
            sa, sb = split(seq((step2a, 0)), 2)
            run(sa)
            run(n1)
            run(sb)
            run(seq((arrive, t, 1), (slots_in, t, 1), (f_add, "C", 1, t), (gather, "C", 1)))
            run(seq((slots, t, 1)))
            weave(seq((slots_k, t, 1)), seq((step2b, 0)))
            m0, m1 = split(seq((mins, "C", 0, 4)), 4)
            run(m0 + m1)
            sa, sb = split(seq((step2a, 1)), 2)
            run(sa)
            run(seq((mins, "O", 0, 4)))
            run(seq((scan, "C", 0), (k_copy, "C", 0)))
            run(sb)
            run(seq((scan, "O", 0), (k_copy, "O", 0), (thr, 0), (swap, 0)))
            ra, rb = split(seq((rest, t, 0)), 10)
            gather("O", 1)
            run(ra)
            m0, m1 = split(seq((step2b, 1), (mins, "O", 1, 2), (mins, "C", 1, 2)), 4 + 16)
            weave(rb, m0)
            c0, c1 = split(m1, 8)
            run(c0 + c1)
            run(seq((scan, "O", 1), (thr, 1)))
            if more:
                run(seq((next_pool, t, 0)))
        k_copy("O", 1)
        scan("C", 1)
        swap(1)
        k_copy("C", 1)
        if more:
            count(t)
            c_ps("O", 0, t)
            if t + 1 < 4:
                d_rep(0)
        R = seq((rest, t, 1))

    r0, R = split(R, 15)
    weave(r0, seq((turn_out, "C", 0), (turn_out, "O", 0)))
    weave(seq((turn_out, "C", 1), (turn_out, "O", 1)), R)
    for l, y, sem in (("C", T.yc, "oc"), ("O", T.yo, "oo")):
        sync("y", ["y%s%d%d" % (l, h, q) for h in range(2) for q in range(2)], [])
        g.sync.dma_start(y[:], T["y" + l][:]).then_inc(T.sem[sem], 16)
    sync("s", ["yd.0", "yd.1"], [])
    g.scalar.dma_start(T.yd[:], T.yd_s[:]).then_inc(T.sem.od, 16)
    for q in "vspg":
        g.wait_ge(S[q], cnt[q])
    g.wait_ge(T.sem.sent, nout * 2 * (NT - 1))
    for sem in ("lxt", "lwr", "lwt", "ldm", "lpo", "lpk", "oc", "oo", "od"):
        g.wait_ge(T.sem[sem], 16)
    for t in range(1, NT):
        for h in range(2):
            g.wait_ge(T.sem["ar%d%d" % (t, h)], nin)
